import numpy as np
import ml_dtypes


def mxq(x, axis, fmt="e4m3"):
    dtype, down = {"e4m3": (ml_dtypes.float8_e4m3fn, 7), "e5m2": (ml_dtypes.float8_e5m2, 14)}[fmt]
    v = np.moveaxis(np.asarray(x, np.float32).astype(ml_dtypes.bfloat16).astype(np.float64), axis, -1)
    blocks = v.reshape(v.shape[:-1] + (-1, 32))
    amax = np.abs(blocks).max(-1, keepdims=True)
    byte = np.maximum(np.where(amax > 0, np.frexp(amax)[1] - 1 + 127, 0) - down, 1)
    scale = np.exp2(byte - 127.0)
    codes = (blocks / scale).astype(np.float32).astype(dtype).astype(np.float64)
    return np.moveaxis((codes * scale).reshape(v.shape), -1, axis)


WIDE = False


def mx_kscale(k):
    if not WIDE:
        return np.ones(k)
    levels = np.array([10, -10, 5, -5, 0])
    if k % 512:
        return np.exp2(np.random.permutation(np.resize(levels, k // 32))).repeat(32)
    a = np.empty((k // 512, 16))
    for p in range(k // 512):
        a[p, :8] = np.random.permutation(np.resize(levels, 8))
        for g in range(8):
            far = levels[np.abs(levels - a[p, g]) >= 10]
            a[p, g + 8] = far[np.random.randint(len(far))]
    return np.exp2(a.ravel()).repeat(32)


def f64(x):
    return np.asarray(x).astype(np.float64)


def striped(idx):
    return np.tile(idx.reshape(-1, 16).T, (8, 1)).astype(np.uint16)


def unstriped(offs):
    return offs[:16].T.reshape(-1).astype(np.int64)


E2M1 = np.array([0.0, 0.5, 1.0, 1.5, 2.0, 3.0, 4.0, 6.0, -0.0, -0.5, -1.0, -1.5, -2.0, -3.0, -4.0, -6.0])


def pack_weight(w, fmt):
    k, n = w.shape
    w = f64(np.asarray(w, np.float32).astype(ml_dtypes.bfloat16)).reshape(k // 32, 32, n)
    amax = np.abs(w).max(1)
    if fmt == "e4m3":
        byte = np.frexp(amax)[1] - 1 + 127 - 7
    else:
        mant, ex = np.frexp(amax / 6.0)
        byte = np.where(mant > 0.5, ex, ex - 1) + 127
    byte = np.clip(np.where(amax > 0, byte, 1), 1, 254)
    scaled = (w * np.exp2(127.0 - byte)[:, None, :]).reshape(k, n).astype(np.float32)
    by_word = np.ascontiguousarray(scaled.reshape(k // 512, 128, 4, n).transpose(0, 1, 3, 2))
    if fmt == "e4m3":
        words = by_word.astype(ml_dtypes.float8_e4m3fn).view(np.uint8)
    else:
        c = by_word.astype(ml_dtypes.float4_e2m1fn).view(np.uint8) & 0xF
        words = (c[..., 0::2] | (c[..., 1::2] << 4)).reshape(k // 512, 128, 2 * n)
    return np.ascontiguousarray(words), np.ascontiguousarray(byte.astype(np.uint8).reshape(k // 512, 16, n))


def unpack_weight(words, scales, fmt):
    g, _, n = scales.shape
    words = np.ascontiguousarray(words).reshape(g, 128, n, -1)
    if fmt == "e4m3":
        vals = words.view(ml_dtypes.float8_e4m3fn).astype(np.float64)
    else:
        nib = np.empty((g, 128, n, 4), np.uint8)
        nib[..., 0::2] = words & 0xF
        nib[..., 1::2] = words >> 4
        vals = E2M1[nib]
    vals = vals * np.repeat(np.exp2(scales.astype(np.float64) - 127.0), 8, axis=1)[..., None]
    return vals.transpose(0, 1, 3, 2).reshape(g * 512, n)


def silu(v):
    return v / (1.0 + np.exp(-np.maximum(v, -700.0)))


K, T, E, C, H, N = 512, 768, 12, 256, 512, 128
TOP = 4


def by_expert(wq, xq):
    return np.concatenate([wq[e].T @ xq[:, e * C:(e + 1) * C] for e in range(E)], axis=1)


def setup_inputs():
    n = np.random.standard_normal
    s = mx_kscale(K)[:, None]
    u = mx_kscale(H)
    deal = np.repeat(np.arange(E), C).reshape(TOP, T)[:, np.random.permutation(T)]
    deal = np.take_along_axis(deal, np.argsort(np.random.rand(TOP, T), axis=0), axis=0)
    for _ in range(8):
        s_, t_ = np.random.permutation(T).reshape(2, -1); r = np.random.randint(TOP, size=T // 2); x, y = deal[r, s_].copy(), deal[r, t_].copy()
        ok = ~((deal[:, s_] == y).any(0) | (deal[:, t_] == x).any(0)); deal[r[ok], s_[ok]] = y[ok]; deal[r[ok], t_[ok]] = x[ok]
    order = np.lexsort((np.random.rand(TOP * T), deal.reshape(-1)))
    slot_token = order % T; pos = np.empty(TOP * T, np.int64); pos[order] = np.arange(TOP * T); pos = pos.reshape(TOP, T)
    g = np.random.uniform(0.5, 1.5, (TOP, T)); g = g / g.sum(0)
    w1 = [pack_weight(m, "e2m1") for m in n((E, K, H)) / np.sqrt(K) / s[None] * u[None, None, :]]
    w2 = [pack_weight(m, "e2m1") for m in n((E, H, N)) / np.sqrt(H) / u[None, :, None]]
    return {
        "xT": (n((K, T)) * s).astype(np.float32),
        "w1_words": np.stack([m[0] for m in w1]),
        "w1_scales": np.stack([m[1] for m in w1]),
        "w2_words": np.stack([m[0] for m in w2]),
        "w2_scales": np.stack([m[1] for m in w2]),
        "gate": np.stack([np.tile(r, (N, 1)) for r in g]).astype(np.float32),
        "offs": striped(slot_token),
        "pos1": striped(pos[0]),
        "pos2": striped(pos[1]),
        "pos3": striped(pos[2]),
        "pos4": striped(pos[3]),
    }


def reference(xT, w1_words, w1_scales, w2_words, w2_scales, gate, offs, pos1, pos2, pos3, pos4):
    idx = unstriped(offs)
    w1 = np.stack([unpack_weight(w1_words[e], w1_scales[e], "e2m1") for e in range(E)])
    w2 = np.stack([unpack_weight(w2_words[e], w2_scales[e], "e2m1") for e in range(E)])
    xq = mxq(f64(xT)[:, idx], 0, "e4m3")
    h = silu(by_expert(w1, xq))
    y = by_expert(w2, mxq(h, 0, "e4m3"))
    return sum(f64(gate[r]) * y[:, unstriped(p)] for r, p in enumerate((pos1, pos2, pos3, pos4)))

@@ -1,0 +1,323 @@
+from contextlib import ExitStack
+
+import concourse.mybir as mybir
+from concourse.masks import make_identity
+
+K, T, E, C, H, N = 512, 768, 12, 256, 512, 128
+TOP = 4
+P = 128
+S = E * C
+FLOPS = 2 * S * (K * H + H * N)
+
+F32 = mybir.dt.float32
+BF16 = mybir.dt.bfloat16
+U32 = mybir.dt.uint32
+I32 = mybir.dt.int32
+U16 = mybir.dt.uint16
+U8 = mybir.dt.uint8
+FP8X4 = mybir.dt.float8_e4m3fn_x4
+FP4X4 = mybir.dt.float4_e2m1fn_x4
+SILU = mybir.ActivationFunctionType.Silu
+MULT = mybir.AluOpType.mult
+ADD = mybir.AluOpType.add
+
+X_CHUNKS = [(0, 256), (256, 256), (512, 128), (640, 128)]
+X_CAST_ON_SCALAR = (0, 2)
+GATHERS = [(0, 128), (128, 128)] + [(a, 256) for a in range(256, S, 256)]
+UNITS = [(2 * e, 2) for e in range(11)] + [(22, 1), (23, 1)]
+Y_BANKS = [(u,) for u in range(13)]
+Y_ON_VECTOR = (9, 10, 11, 12)
+TURNED = (0, 1, 4, 8)
+LOADS = [
+    ("w1", 2, 4),
+    ("x", 0, 0),
+    ("x", 1, 0),
+    ("s1", 0, 4),
+    ("x", 2, 0),
+    ("x", 3, 0),
+    ("offs", 0, 0),
+    ("w1", 0, 2),
+    ("s1", 4, 12),
+    ("s2", 0, 12),
+    ("w2", 0, 4),
+    ("w1", 4, 8),
+    ("w1", 8, 12),
+    ("w2", 4, 12),
+]
+PERMS = [(2, 4), (5, 8), (9, 12)]
+TAIL = [(0, 512), (512, 256)]
+
+
+def tile_moe_tk_mlp_silu_kernel(
+    tc, xT, w1_words, w1_scales, w2_words, w2_scales, gate, offs, pos1, pos2, pos3, pos4, out
+):
+    nc = tc.nc
+    with ExitStack() as ctx:
+        lists = ctx.enter_context(tc.tile_pool(name="lists", bufs=1))
+        keep = ctx.enter_context(tc.tile_pool(name="keep", bufs=1))
+        ring = ctx.enter_context(tc.tile_pool(name="ring", bufs=4))
+        g_ring = ctx.enter_context(tc.tile_pool(name="g_ring", bufs=3))
+        a_psum = ctx.enter_context(tc.psum_pool(name="a_psum", bufs=5))
+        t_psum = ctx.enter_context(tc.psum_pool(name="t_psum", bufs=1))
+        y_psum = ctx.enter_context(tc.psum_pool(name="y_psum", bufs=2))
+
+        warm = keep.tile([P, 1], F32, name="warm")
+        warm_out = keep.tile([P, 1], F32, name="warm_out")
+        nc.vector.memset(warm[:], 0.0)
+        nc.scalar.activation(out=warm_out[:], in_=warm[:], func=SILU)
+
+        raw_s = keep.tile([P, E, H], U8, name="raw_s", align_bytes=64)
+        w1_s = keep.tile([P, E, H], U8, name="w1_s", align_bytes=64)
+        w2_s = keep.tile([P, E, N], U8, name="w2_s", align_bytes=64)
+        for a in range(0, E, 4):
+            nc.vector.memset(raw_s[:, a : a + 4, :].bitcast(I32), 0)
+        nc.vector.memset(w2_s[:].bitcast(I32), 0)
+        x_scales = keep.tile([P, T], U8, name="x_scales", align_bytes=64)
+        nc.gpsimd.memset(x_scales[:], 0)
+        ident = keep.tile([P, P], F32, name="ident")
+        make_identity(nc, ident[:])
+
+        offs_t = lists.tile([P, S // 16], U16, name="offs_t")
+        x_view = xT.rearrange("(p j) t -> p j t", j=4)
+        x_raw = {}
+        raw_w, w2 = {}, {}
+
+        def load(kind, a, b):
+            if kind == "offs":
+                nc.sync.dma_start(offs_t[:], offs)
+            elif kind == "x":
+                raw = keep.tile([P, 4, X_CHUNKS[a][1]], F32, name=f"x_raw{a}")
+                c = X_CHUNKS[a][0]
+                nc.sync.dma_start(raw[:], x_view[:, :, c : c + X_CHUNKS[a][1]])
+                x_raw[a] = raw
+            elif kind == "s1":
+                for q in range(4):
+                    rows = w1_scales[a:b, 0, 4 * q : 4 * q + 4, :].rearrange("e q i -> q e i")
+                    nc.sync.dma_start(raw_s[32 * q : 32 * q + 4, a:b, :].bitcast(I32), rows.bitcast(I32))
+            elif kind == "s2":
+                for q in range(4):
+                    rows = w2_scales[a:b, 0, 4 * q : 4 * q + 4, :].rearrange("e q n -> q e n")
+                    nc.sync.dma_start(w2_s[32 * q : 32 * q + 4, a:b, :].bitcast(I32), rows.bitcast(I32))
+            elif kind == "w1":
+                words = keep.tile([P, b - a, 2 * H], U8, name=f"raw_w{a}", align_bytes=64)
+                nc.sync.dma_start(words[:], w1_words[a:b, 0].rearrange("e p c -> p e c"))
+                for e in range(a, b):
+                    raw_w[e] = (words, e - a)
+            else:
+                words = keep.tile([P, b - a, 2 * N], U8, name=f"w2_{a}", align_bytes=64)
+                nc.sync.dma_start(words[:], w2_words[a:b, 0].rearrange("e p c -> p e c"))
+                for e in range(a, b):
+                    w2[e] = words[:, e - a, :]
+
+        for kind, a, b in LOADS:
+            load(kind, a, b)
+        pos_t = []
+        for r, pos in enumerate((pos1, pos2, pos3, pos4)):
+            lst = lists.tile([P, T // 16], U16, name=f"pos_t{r}")
+            nc.sync.dma_start(lst[:], pos)
+            pos_t.append(lst)
+        gates = []
+        for r in range(TOP):
+            g_t = keep.tile([P, T], F32, name=f"gate_t{r}")
+            nc.sync.dma_start(g_t[:], gate[r])
+            gates.append(g_t)
+
+        w1 = {}
+
+        def permute(a, b):
+            words, at = raw_w[a]
+            n = b - a
+            turned = keep.tile([P, n, 2 * H], U8, name=f"w1_{a}", align_bytes=64)
+            nc.vector.tensor_copy(
+                out=turned[:].bitcast(U16).rearrange("p e (t m) -> p t e m", t=4),
+                in_=words[:, at : at + n, :].bitcast(U16).rearrange("p e (m t) -> p t e m", t=4),
+            )
+            nc.vector.tensor_copy(
+                out=w1_s[:, a:b, :].rearrange("p e (t m) -> p t e m", t=4),
+                in_=raw_s[:, a:b, :].rearrange("p e (m t) -> p t e m", t=4),
+            )
+            for e in range(a, b):
+                w1[e] = turned[:, e - a, :]
+
+        x_words = keep.tile([P, T], U32, name="x_words", align_bytes=64)
+        x_bf = []
+        for i, (a, n) in enumerate(X_CHUNKS):
+            xb = keep.tile([P, n, 4], BF16, name=f"x_bf{i}", align_bytes=64)
+            x_bf.append(xb)
+
+        def cast(i):
+            src = x_raw[i][:].rearrange("p j t -> p t j")
+            if i in X_CAST_ON_SCALAR:
+                nc.scalar.copy(out=x_bf[i][:], in_=src)
+            else:
+                nc.vector.tensor_copy(out=x_bf[i][:], in_=src)
+
+        def quantise_x(i):
+            a, n = X_CHUNKS[i]
+            nc.vector.quantize_mx(
+                out=x_words[:, a : a + n].bitcast(FP8X4),
+                scales=x_scales[:, a : a + n],
+                in_=x_bf[i][:].rearrange("p t j -> p (t j)"),
+            )
+
+        cast(0)
+        cast(1)
+        quantise_x(0)
+        quantise_x(1)
+        cast(2)
+        cast(3)
+        quantise_x(2)
+        quantise_x(3)
+
+        g_words, g_scales = {}, {}
+
+        def gather(i):
+            a, n = GATHERS[i]
+            words = g_ring.tile([P, n], U32, name=f"g_words_{n}", align_bytes=64)
+            nc.vector.tensor_copy(words[:], x_words[:].indirect(offs_t[:, a // 16 : (a + n) // 16]))
+            scales = g_ring.tile([P, n], U8, name=f"g_scales_{n}", align_bytes=64)
+            nc.vector.tensor_copy(scales[:], x_scales[:].indirect(offs_t[:, a // 16 : (a + n) // 16]))
+            for s in range(0, n, P):
+                g_words[(a + s) // P] = words[:, s : s + P]
+                g_scales[(a + s) // P] = scales[:, s : s + P]
+
+        y_all = keep.tile([P, S], F32, name="y_all")
+        h_bf, h_in, h_words, h_scales, y_ps = {}, {}, {}, {}, {}
+
+        def first(unit):
+            g0, count = UNITS[unit]
+            e = g0 // 2
+            if e in TURNED:
+                words, at = raw_w[e]
+                for g in range(g0, g0 + count):
+                    acc = a_psum.tile([P, H], F32, name="acc")
+                    nc.tensor.matmul_mx(
+                        out=acc[:],
+                        lhsT=g_words[g].bitcast(FP8X4),
+                        lhsT_scale=g_scales[g],
+                        rhs=words[:, at, :].bitcast(FP4X4),
+                        rhs_scale=raw_s[:, e, :],
+                        start=True,
+                        stop=True,
+                    )
+                    h = ring.tile([P, H], BF16, name="h", align_bytes=64)
+                    nc.scalar.activation(
+                        out=h[:].rearrange("s (u p e) -> s u p e", u=2, e=2),
+                        in_=acc[:].rearrange("s (p u e) -> s u p e", u=2, e=2),
+                        func=SILU,
+                    )
+                    h_bf[g] = h
+                return
+            hin = ring.tile([P, count * P, 4], BF16, name=f"hin{count}", align_bytes=64)
+            for g in range(count):
+                acc = a_psum.tile([P, 4, P], F32, name="acc")
+                for t in range(4):
+                    nc.tensor.matmul_mx(
+                        out=acc[:, t, :],
+                        lhsT=w1[e][:, 2 * P * t : 2 * P * (t + 1)].bitcast(FP4X4),
+                        lhsT_scale=w1_s[:, e, P * t : P * (t + 1)],
+                        rhs=g_words[g0 + g].bitcast(FP8X4),
+                        rhs_scale=g_scales[g0 + g],
+                        start=True,
+                        stop=True,
+                    )
+                nc.scalar.activation(
+                    out=hin[:, g * P : (g + 1) * P, :],
+                    in_=acc[:].rearrange("p t s -> p s t"),
+                    func=SILU,
+                )
+            h_in[unit] = hin
+
+        def turn(unit):
+            g0, count = UNITS[unit]
+            bank = t_psum.tile([P, 2, 2, P], F32, name="bank")
+            for g in range(count):
+                words = h_bf[g0 + g][:].bitcast(F32)
+                for u in range(2):
+                    nc.tensor.transpose(bank[:, g, u, :], words[:, u * P : (u + 1) * P], ident[:])
+            hin = ring.tile([P, count * P, 4], BF16, name=f"hin{count}", align_bytes=64)
+            nc.scalar.copy(
+                out=hin[:].bitcast(F32).rearrange("p (g r) u -> p g r u", g=count),
+                in_=bank[:, 0:count].rearrange("p g u r -> p g r u"),
+            )
+            h_in[unit] = hin
+
+        def quantise(unit):
+            n = UNITS[unit][1] * P
+            hw = ring.tile([P, n], U32, name=f"hw{n}", align_bytes=64)
+            hs = ring.tile([P, n], U8, name=f"hs{n}", align_bytes=64)
+            nc.vector.quantize_mx(
+                out=hw[:].bitcast(FP8X4), scales=hs[:], in_=h_in[unit][:].rearrange("p s j -> p (s j)")
+            )
+            h_words[unit], h_scales[unit] = hw, hs
+
+        def second(unit):
+            g0, count = UNITS[unit]
+            e = g0 // 2
+            bank = [b for b in Y_BANKS if unit in b][0]
+            if unit == bank[0]:
+                y_ps[bank] = y_psum.tile([P, 512], F32, name="yp")
+            at = (g0 - UNITS[bank[0]][0]) * P
+            nc.tensor.matmul_mx(
+                out=y_ps[bank][:, at : at + count * P],
+                lhsT=w2[e].bitcast(FP4X4),
+                lhsT_scale=w2_s[:, e, :],
+                rhs=h_words[unit][:].bitcast(FP8X4),
+                rhs_scale=h_scales[unit][:],
+                start=True,
+                stop=True,
+            )
+
+        def keep_y(unit):
+            bank = [b for b in Y_BANKS if unit in b][0]
+            if unit == bank[-1]:
+                a = UNITS[bank[0]][0] * P
+                n = sum([UNITS[u][1] for u in bank]) * P
+                if unit in Y_ON_VECTOR:
+                    nc.vector.tensor_copy(out=y_all[:, a : a + n], in_=y_ps[bank][:, 0:n])
+                else:
+                    nc.scalar.copy(out=y_all[:, a : a + n], in_=y_ps[bank][:, 0:n])
+
+        done = 0
+        permuted = 0
+        steps = len(UNITS)
+        for step in range(steps + 3):
+            ahead = UNITS[min(step + 1, steps - 1)][0] * P
+            while done < len(GATHERS) and GATHERS[done][0] <= ahead:
+                gather(done)
+                done += 1
+            while permuted < len(PERMS) and PERMS[permuted][0] <= step + 2:
+                permute(*PERMS[permuted])
+                permuted += 1
+            if step < steps:
+                first(step)
+            if 1 <= step <= steps and UNITS[step - 1][0] // 2 in TURNED:
+                turn(step - 1)
+            if 2 <= step <= steps + 1:
+                quantise(step - 2)
+                second(step - 2)
+            if 3 <= step:
+                keep_y(step - 3)
+
+        prod = []
+        part = keep.tile([P, T], F32, name="part")
+        total = keep.tile([P, T], F32, name="total")
+        res = keep.tile([P, T], F32, name="res")
+
+        def weigh(r):
+            term = keep.tile([P, T], F32, name=f"term{r}")
+            nc.vector.tensor_tensor(term[:], y_all[:].indirect(pos_t[r][:]), gates[r][:], MULT)
+            prod.append(term)
+
+        weigh(0)
+        weigh(1)
+        weigh(2)
+        nc.vector.tensor_tensor(part[:], prod[0][:], prod[1][:], ADD)
+        weigh(3)
+        for a, n in TAIL:
+            cols = slice(a, a + n)
+            nc.vector.tensor_tensor(total[:, cols], part[:, cols], prod[2][:, cols], ADD)
+        for a, n in TAIL:
+            cols = slice(a, a + n)
+            nc.vector.tensor_tensor(res[:, cols], total[:, cols], prod[3][:, cols], ADD)
+            nc.sync.dma_start(out[:, cols], res[:, cols])

@@ -23,29 +23,26 @@ ADD = mybir.AluOpType.add
 
 X_CHUNKS = [(0, 256), (256, 256), (512, 128), (640, 128)]
 X_CAST_ON_SCALAR = (0, 2)
-GATHERS = [(0, 128), (128, 128)] + [(a, 256) for a in range(256, S, 256)]
-UNITS = [(2 * e, 2) for e in range(11)] + [(22, 1), (23, 1)]
-Y_BANKS = [(u,) for u in range(13)]
-Y_ON_VECTOR = (9, 10, 11, 12)
-TURNED = (0, 1, 4, 8)
+UNITS = [(0, 2), (2, 2), (4, 2), (6, 2), (8, 2), (10, 1), (11, 1)]
+Y_BANKS = 3
+Y_ON_VECTOR = (5, 6)
+TURNED = 7
 LOADS = [
-    ("w1", 2, 4),
     ("x", 0, 0),
     ("x", 1, 0),
-    ("s1", 0, 4),
     ("x", 2, 0),
     ("x", 3, 0),
     ("offs", 0, 0),
     ("w1", 0, 2),
+    ("s1", 0, 4),
+    ("w1", 2, 4),
     ("s1", 4, 12),
-    ("s2", 0, 12),
-    ("w2", 0, 4),
     ("w1", 4, 8),
     ("w1", 8, 12),
-    ("w2", 4, 12),
+    ("s2", 0, 12),
+    ("w2", 0, 12),
 ]
-PERMS = [(2, 4), (5, 8), (9, 12)]
-TAIL = [(0, 512), (512, 256)]
+SUM_ON_TENSOR = 512
 
 
 def tile_moe_tk_mlp_silu_kernel(
@@ -55,11 +52,12 @@ def tile_moe_tk_mlp_silu_kernel(
     with ExitStack() as ctx:
         lists = ctx.enter_context(tc.tile_pool(name="lists", bufs=1))
         keep = ctx.enter_context(tc.tile_pool(name="keep", bufs=1))
-        ring = ctx.enter_context(tc.tile_pool(name="ring", bufs=4))
-        g_ring = ctx.enter_context(tc.tile_pool(name="g_ring", bufs=3))
-        a_psum = ctx.enter_context(tc.psum_pool(name="a_psum", bufs=5))
-        t_psum = ctx.enter_context(tc.psum_pool(name="t_psum", bufs=1))
-        y_psum = ctx.enter_context(tc.psum_pool(name="y_psum", bufs=2))
+        ring = ctx.enter_context(tc.tile_pool(name="ring", bufs=6))
+        g_ring = ctx.enter_context(tc.tile_pool(name="g_ring", bufs=6))
+        late = ctx.enter_context(tc.tile_pool(name="late", bufs=1))
+        a_psum = ctx.enter_context(tc.psum_pool(name="a_psum", bufs=3))
+        t_psum = ctx.enter_context(tc.psum_pool(name="t_psum", bufs=2))
+        y_psum = ctx.enter_context(tc.psum_pool(name="y_psum", bufs=Y_BANKS))
 
         warm = keep.tile([P, 1], F32, name="warm")
         warm_out = keep.tile([P, 1], F32, name="warm_out")
@@ -67,7 +65,6 @@ def tile_moe_tk_mlp_silu_kernel(
         nc.scalar.activation(out=warm_out[:], in_=warm[:], func=SILU)
 
         raw_s = keep.tile([P, E, H], U8, name="raw_s", align_bytes=64)
-        w1_s = keep.tile([P, E, H], U8, name="w1_s", align_bytes=64)
         w2_s = keep.tile([P, E, N], U8, name="w2_s", align_bytes=64)
         for a in range(0, E, 4):
             nc.vector.memset(raw_s[:, a : a + 4, :].bitcast(I32), 0)
@@ -92,12 +89,12 @@ def tile_moe_tk_mlp_silu_kernel(
                 x_raw[a] = raw
             elif kind == "s1":
                 for q in range(4):
-                    rows = w1_scales[a:b, 0, 4 * q : 4 * q + 4, :].rearrange("e q i -> q e i")
-                    nc.sync.dma_start(raw_s[32 * q : 32 * q + 4, a:b, :].bitcast(I32), rows.bitcast(I32))
+                    rows = w1_scales[a:b, 0, q:16:4, :].rearrange("e q i -> q e i")
+                    nc.sync.dma_start(raw_s[q:P:32, a:b, :].bitcast(I32), rows.bitcast(I32))
             elif kind == "s2":
                 for q in range(4):
-                    rows = w2_scales[a:b, 0, 4 * q : 4 * q + 4, :].rearrange("e q n -> q e n")
-                    nc.sync.dma_start(w2_s[32 * q : 32 * q + 4, a:b, :].bitcast(I32), rows.bitcast(I32))
+                    rows = w2_scales[a:b, 0, q:16:4, :].rearrange("e q n -> q e n")
+                    nc.sync.dma_start(w2_s[q:P:32, a:b, :].bitcast(I32), rows.bitcast(I32))
             elif kind == "w1":
                 words = keep.tile([P, b - a, 2 * H], U8, name=f"raw_w{a}", align_bytes=64)
                 nc.sync.dma_start(words[:], w1_words[a:b, 0].rearrange("e p c -> p e c"))
@@ -122,22 +119,20 @@ def tile_moe_tk_mlp_silu_kernel(
             nc.sync.dma_start(g_t[:], gate[r])
             gates.append(g_t)
 
-        w1 = {}
+        w1, w1_s = {}, {}
 
-        def permute(a, b):
-            words, at = raw_w[a]
-            n = b - a
-            turned = keep.tile([P, n, 2 * H], U8, name=f"w1_{a}", align_bytes=64)
+        def permute(e):
+            words, at = raw_w[e]
+            w1[e] = keep.tile([P, 2 * H], U8, name=f"w1_words_p{e}", align_bytes=64)
             nc.vector.tensor_copy(
-                out=turned[:].bitcast(U16).rearrange("p e (t m) -> p t e m", t=4),
-                in_=words[:, at : at + n, :].bitcast(U16).rearrange("p e (m t) -> p t e m", t=4),
+                out=w1[e][:].bitcast(U16).rearrange("p (t m) -> p t m", t=4),
+                in_=words[:, at, :].bitcast(U16).rearrange("p (m t) -> p t m", t=4),
             )
+            w1_s[e] = keep.tile([P, H], U8, name=f"w1_scales_p{e}", align_bytes=64)
             nc.vector.tensor_copy(
-                out=w1_s[:, a:b, :].rearrange("p e (t m) -> p t e m", t=4),
-                in_=raw_s[:, a:b, :].rearrange("p e (m t) -> p t e m", t=4),
+                out=w1_s[e][:].rearrange("p (t m) -> p t m", t=4),
+                in_=raw_s[:, e, :].rearrange("p (m t) -> p t m", t=4),
             )
-            for e in range(a, b):
-                w1[e] = turned[:, e - a, :]
 
         x_words = keep.tile([P, T], U32, name="x_words", align_bytes=64)
         x_bf = []
@@ -171,9 +166,11 @@ def tile_moe_tk_mlp_silu_kernel(
 
         g_words, g_scales = {}, {}
 
-        def gather(i):
-            a, n = GATHERS[i]
-            words = g_ring.tile([P, n], U32, name=f"g_words_{n}", align_bytes=64)
+        def gather(a, n):
+            if a + n == S:
+                words = late.tile([P, n], U32, name="g_words_last", align_bytes=64, offset=0)
+            else:
+                words = g_ring.tile([P, n], U32, name=f"g_words_{n}", align_bytes=64)
             nc.vector.tensor_copy(words[:], x_words[:].indirect(offs_t[:, a // 16 : (a + n) // 16]))
             scales = g_ring.tile([P, n], U8, name=f"g_scales_{n}", align_bytes=64)
             nc.vector.tensor_copy(scales[:], x_scales[:].indirect(offs_t[:, a // 16 : (a + n) // 16]))
@@ -182,19 +179,23 @@ def tile_moe_tk_mlp_silu_kernel(
                 g_scales[(a + s) // P] = scales[:, s : s + P]
 
         y_all = keep.tile([P, S], F32, name="y_all")
-        h_bf, h_in, h_words, h_scales, y_ps = {}, {}, {}, {}, {}
+        h_in = [keep.tile([P, n * C, 4], BF16, name=f"h_in{a}", align_bytes=64) for a, n in UNITS]
+        h_bf = {}
 
-        def first(unit):
-            g0, count = UNITS[unit]
-            e = g0 // 2
-            if e in TURNED:
-                words, at = raw_w[e]
-                for g in range(g0, g0 + count):
-                    acc = a_psum.tile([P, H], F32, name="acc")
+        def hidden(e):
+            u = [i for i, (a, n) in enumerate(UNITS) if a <= e < a + n][0]
+            at = (e - UNITS[u][0]) * C
+            return h_in[u][:, at : at + C, :]
+
+        def first(e):
+            for g in range(2):
+                acc = a_psum.tile([P, 4, P], F32, name="acc")
+                if e < TURNED:
+                    words, at = raw_w[e]
                     nc.tensor.matmul_mx(
-                        out=acc[:],
-                        lhsT=g_words[g].bitcast(FP8X4),
-                        lhsT_scale=g_scales[g],
+                        out=acc[:].rearrange("s t m -> s (t m)"),
+                        lhsT=g_words[2 * e + g].bitcast(FP8X4),
+                        lhsT_scale=g_scales[2 * e + g],
                         rhs=words[:, at, :].bitcast(FP4X4),
                         rhs_scale=raw_s[:, e, :],
                         start=True,
@@ -203,121 +204,115 @@ def tile_moe_tk_mlp_silu_kernel(
                     h = ring.tile([P, H], BF16, name="h", align_bytes=64)
                     nc.scalar.activation(
                         out=h[:].rearrange("s (u p e) -> s u p e", u=2, e=2),
-                        in_=acc[:].rearrange("s (p u e) -> s u p e", u=2, e=2),
+                        in_=acc[:].rearrange("s t m -> s (t m)").rearrange("s (p u e) -> s u p e", u=2, e=2),
                         func=SILU,
                     )
-                    h_bf[g] = h
-                return
-            hin = ring.tile([P, count * P, 4], BF16, name=f"hin{count}", align_bytes=64)
-            for g in range(count):
-                acc = a_psum.tile([P, 4, P], F32, name="acc")
-                for t in range(4):
-                    nc.tensor.matmul_mx(
-                        out=acc[:, t, :],
-                        lhsT=w1[e][:, 2 * P * t : 2 * P * (t + 1)].bitcast(FP4X4),
-                        lhsT_scale=w1_s[:, e, P * t : P * (t + 1)],
-                        rhs=g_words[g0 + g].bitcast(FP8X4),
-                        rhs_scale=g_scales[g0 + g],
-                        start=True,
-                        stop=True,
+                    h_bf[2 * e + g] = h
+                else:
+                    for t in range(4):
+                        nc.tensor.matmul_mx(
+                            out=acc[:, t, :],
+                            lhsT=w1[e][:, 2 * P * t : 2 * P * (t + 1)].bitcast(FP4X4),
+                            lhsT_scale=w1_s[e][:, P * t : P * (t + 1)],
+                            rhs=g_words[2 * e + g].bitcast(FP8X4),
+                            rhs_scale=g_scales[2 * e + g],
+                            start=True,
+                            stop=True,
+                        )
+                    nc.scalar.activation(
+                        out=hidden(e)[:, g * P : (g + 1) * P, :],
+                        in_=acc[:].rearrange("p t s -> p s t"),
+                        func=SILU,
                     )
-                nc.scalar.activation(
-                    out=hin[:, g * P : (g + 1) * P, :],
-                    in_=acc[:].rearrange("p t s -> p s t"),
-                    func=SILU,
-                )
-            h_in[unit] = hin
 
-        def turn(unit):
-            g0, count = UNITS[unit]
+        def turn(e):
             bank = t_psum.tile([P, 2, 2, P], F32, name="bank")
-            for g in range(count):
-                words = h_bf[g0 + g][:].bitcast(F32)
+            for g in range(2):
+                words = h_bf[2 * e + g][:].bitcast(F32)
                 for u in range(2):
                     nc.tensor.transpose(bank[:, g, u, :], words[:, u * P : (u + 1) * P], ident[:])
-            hin = ring.tile([P, count * P, 4], BF16, name=f"hin{count}", align_bytes=64)
             nc.scalar.copy(
-                out=hin[:].bitcast(F32).rearrange("p (g r) u -> p g r u", g=count),
-                in_=bank[:, 0:count].rearrange("p g u r -> p g r u"),
+                out=hidden(e).bitcast(F32).rearrange("p (g r) u -> p g r u", g=2),
+                in_=bank[:].rearrange("p g u r -> p g r u"),
             )
-            h_in[unit] = hin
 
-        def quantise(unit):
-            n = UNITS[unit][1] * P
-            hw = ring.tile([P, n], U32, name=f"hw{n}", align_bytes=64)
-            hs = ring.tile([P, n], U8, name=f"hs{n}", align_bytes=64)
+        gather(0, P)
+        gather(P, P)
+        for e in range(E):
+            if e + 1 < E:
+                if e + 1 >= TURNED:
+                    permute(e + 1)
+                gather((e + 1) * C, C)
+            first(e)
+            if 1 <= e <= TURNED:
+                turn(e - 1)
+
+        h_scales = late.tile([P, S], U8, name="h_scales", align_bytes=64, offset=0)
+        for u, (a, n) in enumerate(UNITS):
+            h_words = keep.tile([P, n * C], U32, name=f"h_words{a}", align_bytes=64)
             nc.vector.quantize_mx(
-                out=hw[:].bitcast(FP8X4), scales=hs[:], in_=h_in[unit][:].rearrange("p s j -> p (s j)")
+                out=h_words[:].bitcast(FP8X4),
+                scales=h_scales[:, a * C : (a + n) * C],
+                in_=h_in[u][:].rearrange("p s j -> p (s j)"),
             )
-            h_words[unit], h_scales[unit] = hw, hs
+            if u < Y_BANKS:
+                bank = y_psum.tile([P, 4, P], F32, name="yp")
+            else:
+                bank = a_psum.tile([P, 4, P], F32, name="acc")
+            y_ps = bank[:].rearrange("p a b -> p (a b)")
+            for i in range(n):
+                nc.tensor.matmul_mx(
+                    out=y_ps[:, i * C : (i + 1) * C],
+                    lhsT=w2[a + i].bitcast(FP4X4),
+                    lhsT_scale=w2_s[:, a + i, :],
+                    rhs=h_words[:, i * C : (i + 1) * C].bitcast(FP8X4),
+                    rhs_scale=h_scales[:, (a + i) * C : (a + i + 1) * C],
+                    start=True,
+                    stop=True,
+                )
+            if u in Y_ON_VECTOR:
+                nc.vector.tensor_copy(out=y_all[:, a * C : (a + n) * C], in_=y_ps[:, 0 : n * C])
+            else:
+                nc.scalar.copy(out=y_all[:, a * C : (a + n) * C], in_=y_ps[:, 0 : n * C])
 
-        def second(unit):
-            g0, count = UNITS[unit]
-            e = g0 // 2
-            bank = [b for b in Y_BANKS if unit in b][0]
-            if unit == bank[0]:
-                y_ps[bank] = y_psum.tile([P, 512], F32, name="yp")
-            at = (g0 - UNITS[bank[0]][0]) * P
-            nc.tensor.matmul_mx(
-                out=y_ps[bank][:, at : at + count * P],
-                lhsT=w2[e].bitcast(FP4X4),
-                lhsT_scale=w2_s[:, e, :],
-                rhs=h_words[unit][:].bitcast(FP8X4),
-                rhs_scale=h_scales[unit][:],
-                start=True,
-                stop=True,
+        res = keep.tile([P, SUM_ON_TENSOR], F32, name="res")
+
+        def weigh(r, a, n):
+            term = keep.tile([P, n], F32, name=f"term{r}_{a}")
+            nc.vector.tensor_tensor(
+                term[:], y_all[:].indirect(pos_t[r][:, a // 16 : (a + n) // 16]), gates[r][:, a : a + n], MULT
             )
+            return term
 
-        def keep_y(unit):
-            bank = [b for b in Y_BANKS if unit in b][0]
-            if unit == bank[-1]:
-                a = UNITS[bank[0]][0] * P
-                n = sum([UNITS[u][1] for u in bank]) * P
-                if unit in Y_ON_VECTOR:
-                    nc.vector.tensor_copy(out=y_all[:, a : a + n], in_=y_ps[bank][:, 0:n])
-                else:
-                    nc.scalar.copy(out=y_all[:, a : a + n], in_=y_ps[bank][:, 0:n])
+        blocks = SUM_ON_TENSOR // P
+        sums = [y_psum.tile([P, 4, P], F32, name="yp") for b in range(Y_BANKS)]
+        sums.append(t_psum.tile([P, 4, P], F32, name="bank"))
+        for r in range(TOP):
+            term = weigh(r, 0, SUM_ON_TENSOR)
+            for b in range(blocks):
+                nc.tensor.matmul(
+                    sums[b][:, 0, :],
+                    lhsT=term[:, b * P : (b + 1) * P],
+                    rhs=ident[:],
+                    is_transpose=True,
+                    start=r == 0,
+                    stop=r == TOP - 1,
+                )
+        back = t_psum.tile([P, 512], F32, name="bank")
+        for b in range(blocks):
+            sum_t = keep.tile([P, P], F32, name=f"sum_t{b}")
+            nc.scalar.copy(out=sum_t[:], in_=sums[b][:, 0, :])
+            nc.tensor.transpose(back[:, b * P : (b + 1) * P], sum_t[:], ident[:])
+        nc.scalar.copy(out=res[:, 0:SUM_ON_TENSOR], in_=back[:, 0:SUM_ON_TENSOR])
+        nc.sync.dma_start(out[:, 0:SUM_ON_TENSOR], res[:, 0:SUM_ON_TENSOR])
 
-        done = 0
-        permuted = 0
-        steps = len(UNITS)
-        for step in range(steps + 3):
-            ahead = UNITS[min(step + 1, steps - 1)][0] * P
-            while done < len(GATHERS) and GATHERS[done][0] <= ahead:
-                gather(done)
-                done += 1
-            while permuted < len(PERMS) and PERMS[permuted][0] <= step + 2:
-                permute(*PERMS[permuted])
-                permuted += 1
-            if step < steps:
-                first(step)
-            if 1 <= step <= steps and UNITS[step - 1][0] // 2 in TURNED:
-                turn(step - 1)
-            if 2 <= step <= steps + 1:
-                quantise(step - 2)
-                second(step - 2)
-            if 3 <= step:
-                keep_y(step - 3)
-
-        prod = []
-        part = keep.tile([P, T], F32, name="part")
-        total = keep.tile([P, T], F32, name="total")
-        res = keep.tile([P, T], F32, name="res")
-
-        def weigh(r):
-            term = keep.tile([P, T], F32, name=f"term{r}")
-            nc.vector.tensor_tensor(term[:], y_all[:].indirect(pos_t[r][:]), gates[r][:], MULT)
-            prod.append(term)
-
-        weigh(0)
-        weigh(1)
-        weigh(2)
+        rest = T - SUM_ON_TENSOR
+        part = keep.tile([P, rest], F32, name="part")
+        total = keep.tile([P, rest], F32, name="total")
+        last = keep.tile([P, rest], F32, name="last")
+        prod = [weigh(r, SUM_ON_TENSOR, rest) for r in range(3)]
         nc.vector.tensor_tensor(part[:], prod[0][:], prod[1][:], ADD)
-        weigh(3)
-        for a, n in TAIL:
-            cols = slice(a, a + n)
-            nc.vector.tensor_tensor(total[:, cols], part[:, cols], prod[2][:, cols], ADD)
-        for a, n in TAIL:
-            cols = slice(a, a + n)
-            nc.vector.tensor_tensor(res[:, cols], total[:, cols], prod[3][:, cols], ADD)
-            nc.sync.dma_start(out[:, cols], res[:, cols])
+        prod.append(weigh(3, SUM_ON_TENSOR, rest))
+        nc.vector.tensor_tensor(total[:], part[:], prod[2][:], ADD)
+        nc.vector.tensor_tensor(last[:], total[:], prod[3][:], ADD)
+        nc.sync.dma_start(out[:, SUM_ON_TENSOR:T], last[:])

@@ -22,7 +22,7 @@ MULT = mybir.AluOpType.mult
 ADD = mybir.AluOpType.add
 
 X_CHUNKS = [(0, 256), (256, 256), (512, 128), (640, 128)]
-X_CAST_ON_SCALAR = (0, 2)
+X_ON_VECTOR = (128, 128, 80, 80)
 UNITS = [(0, 2), (2, 2), (4, 2), (6, 2), (8, 2), (10, 1), (11, 1)]
 Y_BANKS = 3
 Y_ON_VECTOR = (5, 6)
@@ -32,17 +32,17 @@ LOADS = [
     ("x", 1, 0),
     ("x", 2, 0),
     ("x", 3, 0),
+    ("s1", 0, 2),
     ("offs", 0, 0),
     ("w1", 0, 2),
-    ("s1", 0, 4),
     ("w1", 2, 4),
-    ("s1", 4, 12),
+    ("s1", 2, 12),
     ("w1", 4, 8),
     ("w1", 8, 12),
     ("s2", 0, 12),
     ("w2", 0, 12),
 ]
-SUM_ON_TENSOR = 512
+EARLY = 256
 
 
 def tile_moe_tk_mlp_silu_kernel(
@@ -66,8 +66,8 @@ def tile_moe_tk_mlp_silu_kernel(
 
         raw_s = keep.tile([P, E, H], U8, name="raw_s", align_bytes=64)
         w2_s = keep.tile([P, E, N], U8, name="w2_s", align_bytes=64)
-        for a in range(0, E, 4):
-            nc.vector.memset(raw_s[:, a : a + 4, :].bitcast(I32), 0)
+        for a, b in ((0, 2), (2, E)):
+            nc.vector.memset(raw_s[:, a:b, :].bitcast(I32), 0)
         nc.vector.memset(w2_s[:].bitcast(I32), 0)
         x_scales = keep.tile([P, T], U8, name="x_scales", align_bytes=64)
         nc.gpsimd.memset(x_scales[:], 0)
@@ -142,10 +142,9 @@ def tile_moe_tk_mlp_silu_kernel(
 
         def cast(i):
             src = x_raw[i][:].rearrange("p j t -> p t j")
-            if i in X_CAST_ON_SCALAR:
-                nc.scalar.copy(out=x_bf[i][:], in_=src)
-            else:
-                nc.vector.tensor_copy(out=x_bf[i][:], in_=src)
+            cut = X_ON_VECTOR[i]
+            nc.vector.tensor_copy(out=x_bf[i][:, 0:cut, :], in_=src[:, 0:cut, :])
+            nc.scalar.copy(out=x_bf[i][:, cut:, :], in_=src[:, cut:, :])
 
         def quantise_x(i):
             a, n = X_CHUNKS[i]
@@ -155,19 +154,14 @@ def tile_moe_tk_mlp_silu_kernel(
                 in_=x_bf[i][:].rearrange("p t j -> p (t j)"),
             )
 
-        cast(0)
-        cast(1)
-        quantise_x(0)
-        quantise_x(1)
-        cast(2)
-        cast(3)
-        quantise_x(2)
-        quantise_x(3)
+        for i in range(len(X_CHUNKS)):
+            cast(i)
+            quantise_x(i)
 
         g_words, g_scales = {}, {}
 
         def gather(a, n):
-            if a + n == S:
+            if a + n == S - C:
                 words = late.tile([P, n], U32, name="g_words_last", align_bytes=64, offset=0)
             else:
                 words = g_ring.tile([P, n], U32, name=f"g_words_{n}", align_bytes=64)
@@ -275,8 +269,6 @@ def tile_moe_tk_mlp_silu_kernel(
             else:
                 nc.scalar.copy(out=y_all[:, a * C : (a + n) * C], in_=y_ps[:, 0 : n * C])
 
-        res = keep.tile([P, SUM_ON_TENSOR], F32, name="res")
-
         def weigh(r, a, n):
             term = keep.tile([P, n], F32, name=f"term{r}_{a}")
             nc.vector.tensor_tensor(
@@ -284,35 +276,43 @@ def tile_moe_tk_mlp_silu_kernel(
             )
             return term
 
-        blocks = SUM_ON_TENSOR // P
-        sums = [y_psum.tile([P, 4, P], F32, name="yp") for b in range(Y_BANKS)]
-        sums.append(t_psum.tile([P, 4, P], F32, name="bank"))
-        for r in range(TOP):
-            term = weigh(r, 0, SUM_ON_TENSOR)
-            for b in range(blocks):
+        blocks = T // P
+        sums = [a_psum.tile([P, 4, P], F32, name="acc") for b in range(3)]
+        sums += [y_psum.tile([P, 4, P], F32, name="yp") for b in range(3)]
+
+        def add_turned(r, a, n, last):
+            term = weigh(r, a, n)
+            for b in range(a // P, (a + n) // P):
                 nc.tensor.matmul(
                     sums[b][:, 0, :],
-                    lhsT=term[:, b * P : (b + 1) * P],
+                    lhsT=term[:, b * P - a : (b + 1) * P - a],
                     rhs=ident[:],
                     is_transpose=True,
                     start=r == 0,
-                    stop=r == TOP - 1,
+                    stop=r == last,
                 )
-        back = t_psum.tile([P, 512], F32, name="bank")
-        for b in range(blocks):
-            sum_t = keep.tile([P, P], F32, name=f"sum_t{b}")
-            nc.scalar.copy(out=sum_t[:], in_=sums[b][:, 0, :])
-            nc.tensor.transpose(back[:, b * P : (b + 1) * P], sum_t[:], ident[:])
-        nc.scalar.copy(out=res[:, 0:SUM_ON_TENSOR], in_=back[:, 0:SUM_ON_TENSOR])
-        nc.sync.dma_start(out[:, 0:SUM_ON_TENSOR], res[:, 0:SUM_ON_TENSOR])
 
-        rest = T - SUM_ON_TENSOR
-        part = keep.tile([P, rest], F32, name="part")
-        total = keep.tile([P, rest], F32, name="total")
-        last = keep.tile([P, rest], F32, name="last")
-        prod = [weigh(r, SUM_ON_TENSOR, rest) for r in range(3)]
-        nc.vector.tensor_tensor(part[:], prod[0][:], prod[1][:], ADD)
-        prod.append(weigh(3, SUM_ON_TENSOR, rest))
-        nc.vector.tensor_tensor(total[:], part[:], prod[2][:], ADD)
-        nc.vector.tensor_tensor(last[:], total[:], prod[3][:], ADD)
-        nc.sync.dma_start(out[:, SUM_ON_TENSOR:T], last[:])
+        def turn_back(a, n):
+            back = t_psum.tile([P, 512], F32, name="bank")
+            for b in range(a // P, (a + n) // P):
+                sum_t = keep.tile([P, P], F32, name=f"sum_t{b}")
+                nc.scalar.copy(out=sum_t[:], in_=sums[b][:, 0, :])
+                nc.tensor.transpose(back[:, b * P - a : (b + 1) * P - a], sum_t[:], ident[:])
+            return back
+
+        rest = T - EARLY
+        add_turned(0, 0, T, 3)
+        add_turned(1, 0, T, 3)
+        add_turned(2, EARLY, rest, 2)
+        three = turn_back(EARLY, rest)
+        add_turned(2, 0, EARLY, 3)
+        add_turned(3, 0, EARLY, 3)
+        four = turn_back(0, EARLY)
+        res = keep.tile([P, EARLY], F32, name="res")
+        nc.scalar.copy(out=res[:], in_=four[:, 0:EARLY])
+        nc.sync.dma_start(out[:, 0:EARLY], res[:])
+        term = weigh(3, EARLY, rest)
+        for a in range(0, rest, C):
+            last = keep.tile([P, C], F32, name=f"last{a}")
+            nc.vector.tensor_tensor(last[:], term[:, a : a + C], three[:, a : a + C], ADD)
+            nc.sync.dma_start(out[:, EARLY + a : EARLY + a + C], last[:])

@@ -25,8 +25,8 @@ X_CHUNKS = [(0, 256), (256, 256), (512, 128), (640, 128)]
 X_ON_VECTOR = (128, 128, 80, 80)
 UNITS = [(0, 2), (2, 2), (4, 2), (6, 2), (8, 2), (10, 1), (11, 1)]
 Y_BANKS = 3
-Y_ON_VECTOR = (5, 6)
-TURNED = 7
+Y_ON_VECTOR = (4, 5, 6)
+TURNED = 3
 LOADS = [
     ("x", 0, 0),
     ("x", 1, 0),
@@ -124,12 +124,12 @@ def tile_moe_tk_mlp_silu_kernel(
         def permute(e):
             words, at = raw_w[e]
             w1[e] = keep.tile([P, 2 * H], U8, name=f"w1_words_p{e}", align_bytes=64)
-            nc.vector.tensor_copy(
+            nc.gpsimd.tensor_copy(
                 out=w1[e][:].bitcast(U16).rearrange("p (t m) -> p t m", t=4),
                 in_=words[:, at, :].bitcast(U16).rearrange("p (m t) -> p t m", t=4),
             )
             w1_s[e] = keep.tile([P, H], U8, name=f"w1_scales_p{e}", align_bytes=64)
-            nc.vector.tensor_copy(
+            nc.gpsimd.tensor_copy(
                 out=w1_s[e][:].rearrange("p (t m) -> p t m", t=4),
                 in_=raw_s[:, e, :].rearrange("p (m t) -> p t m", t=4),
             )
@@ -161,7 +161,7 @@ def tile_moe_tk_mlp_silu_kernel(
         g_words, g_scales = {}, {}
 
         def gather(a, n):
-            if a + n == S - C:
+            if a + n == S - 2 * C:
                 words = late.tile([P, n], U32, name="g_words_last", align_bytes=64, offset=0)
             else:
                 words = g_ring.tile([P, n], U32, name=f"g_words_{n}", align_bytes=64)

@@ -23,26 +23,29 @@ ADD = mybir.AluOpType.add
 
 X_CHUNKS = [(0, 256), (256, 256), (512, 128), (640, 128)]
 X_ON_VECTOR = (128, 128, 80, 80)
-UNITS = [(0, 2), (2, 2), (4, 2), (6, 2), (8, 2), (10, 1), (11, 1)]
-Y_BANKS = 3
-Y_ON_VECTOR = (4, 5, 6)
+UNITS = [(0, 2), (2, 2), (4, 2), (6, 2), (8, 1), (9, 1), (10, 1), (11, 1)]
+Y_BANKS = 5
+Y_ON_VECTOR = (5, 6, 7)
 TURNED = 3
 LOADS = [
     ("x", 0, 0),
     ("x", 1, 0),
     ("x", 2, 0),
     ("x", 3, 0),
-    ("s1", 0, 2),
+    ("s1", 0, 3),
     ("offs", 0, 0),
     ("w1", 0, 2),
     ("w1", 2, 4),
-    ("s1", 2, 12),
-    ("w1", 4, 8),
+    ("s1", 3, 7),
+    ("w1", 4, 6),
+    ("w1", 6, 8),
+    ("s1", 7, 12),
     ("w1", 8, 12),
     ("s2", 0, 12),
     ("w2", 0, 12),
 ]
-EARLY = 256
+BANK_TOKENS = [(0, 512), (512, 256)]
+STORES = [(0, 256), (256, 256), (512, 256)]
 
 
 def tile_moe_tk_mlp_silu_kernel(
@@ -56,7 +59,6 @@ def tile_moe_tk_mlp_silu_kernel(
         g_ring = ctx.enter_context(tc.tile_pool(name="g_ring", bufs=6))
         late = ctx.enter_context(tc.tile_pool(name="late", bufs=1))
         a_psum = ctx.enter_context(tc.psum_pool(name="a_psum", bufs=3))
-        t_psum = ctx.enter_context(tc.psum_pool(name="t_psum", bufs=2))
         y_psum = ctx.enter_context(tc.psum_pool(name="y_psum", bufs=Y_BANKS))
 
         warm = keep.tile([P, 1], F32, name="warm")
@@ -64,11 +66,8 @@ def tile_moe_tk_mlp_silu_kernel(
         nc.vector.memset(warm[:], 0.0)
         nc.scalar.activation(out=warm_out[:], in_=warm[:], func=SILU)
 
-        raw_s = keep.tile([P, E, H], U8, name="raw_s", align_bytes=64)
+        raw_s = {}
         w2_s = keep.tile([P, E, N], U8, name="w2_s", align_bytes=64)
-        for a, b in ((0, 2), (2, E)):
-            nc.vector.memset(raw_s[:, a:b, :].bitcast(I32), 0)
-        nc.vector.memset(w2_s[:].bitcast(I32), 0)
         x_scales = keep.tile([P, T], U8, name="x_scales", align_bytes=64)
         nc.gpsimd.memset(x_scales[:], 0)
         ident = keep.tile([P, P], F32, name="ident")
@@ -88,10 +87,15 @@ def tile_moe_tk_mlp_silu_kernel(
                 nc.sync.dma_start(raw[:], x_view[:, :, c : c + X_CHUNKS[a][1]])
                 x_raw[a] = raw
             elif kind == "s1":
+                plane = keep.tile([P, b - a, H], U8, name=f"raw_s{a}", align_bytes=64)
+                nc.vector.memset(plane[:].bitcast(I32), 0)
+                for e in range(a, b):
+                    raw_s[e] = plane[:, e - a, :]
                 for q in range(4):
                     rows = w1_scales[a:b, 0, q:16:4, :].rearrange("e q i -> q e i")
-                    nc.sync.dma_start(raw_s[q:P:32, a:b, :].bitcast(I32), rows.bitcast(I32))
+                    nc.sync.dma_start(plane[q:P:32].bitcast(I32), rows.bitcast(I32))
             elif kind == "s2":
+                nc.vector.memset(w2_s[:].bitcast(I32), 0)
                 for q in range(4):
                     rows = w2_scales[a:b, 0, q:16:4, :].rearrange("e q n -> q e n")
                     nc.sync.dma_start(w2_s[q:P:32, a:b, :].bitcast(I32), rows.bitcast(I32))
@@ -131,7 +135,7 @@ def tile_moe_tk_mlp_silu_kernel(
             w1_s[e] = keep.tile([P, H], U8, name=f"w1_scales_p{e}", align_bytes=64)
             nc.gpsimd.tensor_copy(
                 out=w1_s[e][:].rearrange("p (t m) -> p t m", t=4),
-                in_=raw_s[:, e, :].rearrange("p (m t) -> p t m", t=4),
+                in_=raw_s[e].rearrange("p (m t) -> p t m", t=4),
             )
 
         x_words = keep.tile([P, T], U32, name="x_words", align_bytes=64)
@@ -191,7 +195,7 @@ def tile_moe_tk_mlp_silu_kernel(
                         lhsT=g_words[2 * e + g].bitcast(FP8X4),
                         lhsT_scale=g_scales[2 * e + g],
                         rhs=words[:, at, :].bitcast(FP4X4),
-                        rhs_scale=raw_s[:, e, :],
+                        rhs_scale=raw_s[e],
                         start=True,
                         stop=True,
                     )
@@ -220,7 +224,7 @@ def tile_moe_tk_mlp_silu_kernel(
                     )
 
         def turn(e):
-            bank = t_psum.tile([P, 2, 2, P], F32, name="bank")
+            bank = y_psum.tile([P, 2, 2, P], F32, name="yp")
             for g in range(2):
                 words = h_bf[2 * e + g][:].bitcast(F32)
                 for u in range(2):
@@ -293,26 +297,24 @@ def tile_moe_tk_mlp_silu_kernel(
                 )
 
         def turn_back(a, n):
-            back = t_psum.tile([P, 512], F32, name="bank")
+            back = y_psum.tile([P, 512], F32, name="yp")
             for b in range(a // P, (a + n) // P):
                 sum_t = keep.tile([P, P], F32, name=f"sum_t{b}")
                 nc.scalar.copy(out=sum_t[:], in_=sums[b][:, 0, :])
                 nc.tensor.transpose(back[:, b * P - a : (b + 1) * P - a], sum_t[:], ident[:])
             return back
 
-        rest = T - EARLY
-        add_turned(0, 0, T, 3)
-        add_turned(1, 0, T, 3)
-        add_turned(2, EARLY, rest, 2)
-        three = turn_back(EARLY, rest)
-        add_turned(2, 0, EARLY, 3)
-        add_turned(3, 0, EARLY, 3)
-        four = turn_back(0, EARLY)
-        res = keep.tile([P, EARLY], F32, name="res")
-        nc.scalar.copy(out=res[:], in_=four[:, 0:EARLY])
-        nc.sync.dma_start(out[:, 0:EARLY], res[:])
-        term = weigh(3, EARLY, rest)
-        for a in range(0, rest, C):
-            last = keep.tile([P, C], F32, name=f"last{a}")
-            nc.vector.tensor_tensor(last[:], term[:, a : a + C], three[:, a : a + C], ADD)
-            nc.sync.dma_start(out[:, EARLY + a : EARLY + a + C], last[:])
+        add_turned(0, 0, T, 2)
+        add_turned(1, 0, T, 2)
+        three = {}
+        for a, n in BANK_TOKENS:
+            add_turned(2, a, n, 2)
+            three[a] = turn_back(a, n)
+        term = weigh(3, 0, T)
+        for a, n in STORES:
+            first_token = a // 512 * 512
+            last = keep.tile([P, n], F32, name=f"last{a}")
+            nc.vector.tensor_tensor(
+                last[:], term[:, a : a + n], three[first_token][:, a - first_token : a - first_token + n], ADD
+            )
+            nc.sync.dma_start(out[:, a : a + n], last[:])

@@ -23,26 +23,29 @@ ADD = mybir.AluOpType.add
 
 X_CHUNKS = [(0, 256), (256, 256), (512, 128), (640, 128)]
 X_ON_VECTOR = (128, 128, 80, 80)
-UNITS = [(0, 2), (2, 2), (4, 2), (6, 2), (8, 1), (9, 1), (10, 1), (11, 1)]
-Y_BANKS = 5
-Y_ON_VECTOR = (5, 6, 7)
-TURNED = 3
+UNITS = [(0, 2), (2, 2), (4, 2), (6, 2), (8, 2), (10, 1), (11, 1)]
+Y_ON_VECTOR = (4,)
+PACKS = [(0, 8), (8, 4)]
+LIVE_ROWS = 100
 LOADS = [
     ("x", 0, 0),
+    ("pack", 0, 0),
     ("x", 1, 0),
     ("x", 2, 0),
     ("x", 3, 0),
-    ("s1", 0, 3),
     ("offs", 0, 0),
-    ("w1", 0, 2),
-    ("w1", 2, 4),
-    ("s1", 3, 7),
-    ("w1", 4, 6),
-    ("w1", 6, 8),
-    ("s1", 7, 12),
-    ("w1", 8, 12),
+    ("w1", 0, 1),
+    ("w1", 1, 3),
+    ("shift", 1, 3),
+    ("w1", 3, 6),
+    ("shift", 3, 6),
+    ("pack", 1, 0),
+    ("w1", 6, 9),
+    ("shift", 6, 8),
+    ("w1", 9, 12),
     ("s2", 0, 12),
     ("w2", 0, 12),
+    ("shift", 9, 12),
 ]
 BANK_TOKENS = [(0, 512), (512, 256)]
 STORES = [(0, 256), (256, 256), (512, 256)]
@@ -55,18 +58,15 @@ def tile_moe_tk_mlp_silu_kernel(
     with ExitStack() as ctx:
         lists = ctx.enter_context(tc.tile_pool(name="lists", bufs=1))
         keep = ctx.enter_context(tc.tile_pool(name="keep", bufs=1))
-        ring = ctx.enter_context(tc.tile_pool(name="ring", bufs=6))
-        g_ring = ctx.enter_context(tc.tile_pool(name="g_ring", bufs=6))
         late = ctx.enter_context(tc.tile_pool(name="late", bufs=1))
-        a_psum = ctx.enter_context(tc.psum_pool(name="a_psum", bufs=3))
-        y_psum = ctx.enter_context(tc.psum_pool(name="y_psum", bufs=Y_BANKS))
+        psum = ctx.enter_context(tc.psum_pool(name="psum", bufs=8))
 
         warm = keep.tile([P, 1], F32, name="warm")
         warm_out = keep.tile([P, 1], F32, name="warm_out")
         nc.vector.memset(warm[:], 0.0)
         nc.scalar.activation(out=warm_out[:], in_=warm[:], func=SILU)
 
-        raw_s = {}
+        w1_s, packs = {}, {}
         w2_s = keep.tile([P, E, N], U8, name="w2_s", align_bytes=64)
         x_scales = keep.tile([P, T], U8, name="x_scales", align_bytes=64)
         nc.gpsimd.memset(x_scales[:], 0)
@@ -86,14 +86,30 @@ def tile_moe_tk_mlp_silu_kernel(
                 c = X_CHUNKS[a][0]
                 nc.sync.dma_start(raw[:], x_view[:, :, c : c + X_CHUNKS[a][1]])
                 x_raw[a] = raw
-            elif kind == "s1":
-                plane = keep.tile([P, b - a, H], U8, name=f"raw_s{a}", align_bytes=64)
-                nc.vector.memset(plane[:].bitcast(I32), 0)
-                for e in range(a, b):
-                    raw_s[e] = plane[:, e - a, :]
+            elif kind == "pack":
+                e0, count = PACKS[a]
+                raw = keep.tile([P, H], U8, name=f"raw_pack{a}", align_bytes=64)
+                if count < 8:
+                    nc.vector.memset(raw[:].bitcast(I32), 0)
                 for q in range(4):
-                    rows = w1_scales[a:b, 0, q:16:4, :].rearrange("e q i -> q e i")
-                    nc.sync.dma_start(plane[q:P:32].bitcast(I32), rows.bitcast(I32))
+                    rows = w1_scales[e0 : e0 + count, 0, 4 * q : 4 * q + 4, :]
+                    nc.sync.dma_start(raw[32 * q : 32 * q + 4 * count].bitcast(I32), rows.bitcast(I32))
+                packs[a] = keep.tile([P, H], U8, name=f"pack{a}", align_bytes=64)
+                engine = nc.vector if a == 0 else nc.gpsimd
+                engine.tensor_copy(
+                    out=packs[a][:].rearrange("p (t m) -> p t m", t=4),
+                    in_=raw[:].rearrange("p (m t) -> p t m", t=4),
+                )
+                w1_s[e0] = packs[a]
+            elif kind == "shift":
+                for e in range(a, b):
+                    plane = keep.tile([P, H], U8, name=f"w1_plane{e}", align_bytes=64)
+                    nc.vector.memset(plane[:].bitcast(I32), 0)
+                    j = e % 8
+                    nc.sync.dma_start(
+                        plane[0:LIVE_ROWS].bitcast(I32), packs[e // 8][4 * j : 4 * j + LIVE_ROWS].bitcast(I32)
+                    )
+                    w1_s[e] = plane
             elif kind == "s2":
                 nc.vector.memset(w2_s[:].bitcast(I32), 0)
                 for q in range(4):
@@ -123,25 +139,26 @@ def tile_moe_tk_mlp_silu_kernel(
             nc.sync.dma_start(g_t[:], gate[r])
             gates.append(g_t)
 
-        w1, w1_s = {}, {}
+        w1 = {}
 
         def permute(e):
             words, at = raw_w[e]
-            w1[e] = keep.tile([P, 2 * H], U8, name=f"w1_words_p{e}", align_bytes=64)
+            if e == 0:
+                w1[e] = late.tile([P, 2 * H], U8, name="w1_words_first", align_bytes=64, offset=0)
+            else:
+                w1[e] = keep.tile([P, 2 * H], U8, name=f"w1_words_p{e}", align_bytes=64)
             nc.gpsimd.tensor_copy(
                 out=w1[e][:].bitcast(U16).rearrange("p (t m) -> p t m", t=4),
                 in_=words[:, at, :].bitcast(U16).rearrange("p (m t) -> p t m", t=4),
-            )
-            w1_s[e] = keep.tile([P, H], U8, name=f"w1_scales_p{e}", align_bytes=64)
-            nc.gpsimd.tensor_copy(
-                out=w1_s[e][:].rearrange("p (t m) -> p t m", t=4),
-                in_=raw_s[e].rearrange("p (m t) -> p t m", t=4),
             )
 
         x_words = keep.tile([P, T], U32, name="x_words", align_bytes=64)
         x_bf = []
         for i, (a, n) in enumerate(X_CHUNKS):
-            xb = keep.tile([P, n, 4], BF16, name=f"x_bf{i}", align_bytes=64)
+            if i == len(X_CHUNKS) - 1:
+                xb = late.tile([P, n, 4], BF16, name=f"x_bf{i}", align_bytes=64, offset=0)
+            else:
+                xb = keep.tile([P, n, 4], BF16, name=f"x_bf{i}", align_bytes=64)
             x_bf.append(xb)
 
         def cast(i):
@@ -165,98 +182,62 @@ def tile_moe_tk_mlp_silu_kernel(
         g_words, g_scales = {}, {}
 
         def gather(a, n):
-            if a + n == S - 2 * C:
-                words = late.tile([P, n], U32, name="g_words_last", align_bytes=64, offset=0)
-            else:
-                words = g_ring.tile([P, n], U32, name=f"g_words_{n}", align_bytes=64)
+            words = keep.tile([P, n], U32, name=f"g_words_{a}", align_bytes=64)
             nc.vector.tensor_copy(words[:], x_words[:].indirect(offs_t[:, a // 16 : (a + n) // 16]))
-            scales = g_ring.tile([P, n], U8, name=f"g_scales_{n}", align_bytes=64)
+            scales = keep.tile([P, n], U8, name=f"g_scales_{a}", align_bytes=64)
             nc.vector.tensor_copy(scales[:], x_scales[:].indirect(offs_t[:, a // 16 : (a + n) // 16]))
             for s in range(0, n, P):
                 g_words[(a + s) // P] = words[:, s : s + P]
                 g_scales[(a + s) // P] = scales[:, s : s + P]
 
-        y_all = keep.tile([P, S], F32, name="y_all")
-        h_in = [keep.tile([P, n * C, 4], BF16, name=f"h_in{a}", align_bytes=64) for a, n in UNITS]
-        h_bf = {}
+        y_all = keep.tile([P, S], F32, name="y_all", align_bytes=64)
+        h_in = [keep.tile([P, n * C * 4], BF16, name=f"h_in{a}", align_bytes=64)[:] for a, n in UNITS[:-1]]
+        h_in.append(y_all[:, 8 * C : 10 * C].bitcast(BF16))
 
         def hidden(e):
             u = [i for i, (a, n) in enumerate(UNITS) if a <= e < a + n][0]
             at = (e - UNITS[u][0]) * C
-            return h_in[u][:, at : at + C, :]
+            return h_in[u][:, 4 * at : 4 * (at + C)].rearrange("p (s j) -> p s j", j=4)
 
         def first(e):
             for g in range(2):
-                acc = a_psum.tile([P, 4, P], F32, name="acc")
-                if e < TURNED:
-                    words, at = raw_w[e]
+                acc = psum.tile([P, 4, P], F32, name="acc")
+                for t in range(4):
                     nc.tensor.matmul_mx(
-                        out=acc[:].rearrange("s t m -> s (t m)"),
-                        lhsT=g_words[2 * e + g].bitcast(FP8X4),
-                        lhsT_scale=g_scales[2 * e + g],
-                        rhs=words[:, at, :].bitcast(FP4X4),
-                        rhs_scale=raw_s[e],
+                        out=acc[:, t, :],
+                        lhsT=w1[e][:, 2 * P * t : 2 * P * (t + 1)].bitcast(FP4X4),
+                        lhsT_scale=w1_s[e][:, P * t : P * (t + 1)],
+                        rhs=g_words[2 * e + g].bitcast(FP8X4),
+                        rhs_scale=g_scales[2 * e + g],
                         start=True,
                         stop=True,
                     )
-                    h = ring.tile([P, H], BF16, name="h", align_bytes=64)
-                    nc.scalar.activation(
-                        out=h[:].rearrange("s (u p e) -> s u p e", u=2, e=2),
-                        in_=acc[:].rearrange("s t m -> s (t m)").rearrange("s (p u e) -> s u p e", u=2, e=2),
-                        func=SILU,
-                    )
-                    h_bf[2 * e + g] = h
-                else:
-                    for t in range(4):
-                        nc.tensor.matmul_mx(
-                            out=acc[:, t, :],
-                            lhsT=w1[e][:, 2 * P * t : 2 * P * (t + 1)].bitcast(FP4X4),
-                            lhsT_scale=w1_s[e][:, P * t : P * (t + 1)],
-                            rhs=g_words[2 * e + g].bitcast(FP8X4),
-                            rhs_scale=g_scales[2 * e + g],
-                            start=True,
-                            stop=True,
-                        )
-                    nc.scalar.activation(
-                        out=hidden(e)[:, g * P : (g + 1) * P, :],
-                        in_=acc[:].rearrange("p t s -> p s t"),
-                        func=SILU,
-                    )
-
-        def turn(e):
-            bank = y_psum.tile([P, 2, 2, P], F32, name="yp")
-            for g in range(2):
-                words = h_bf[2 * e + g][:].bitcast(F32)
-                for u in range(2):
-                    nc.tensor.transpose(bank[:, g, u, :], words[:, u * P : (u + 1) * P], ident[:])
-            nc.scalar.copy(
-                out=hidden(e).bitcast(F32).rearrange("p (g r) u -> p g r u", g=2),
-                in_=bank[:].rearrange("p g u r -> p g r u"),
-            )
+                nc.scalar.activation(
+                    out=hidden(e)[:, g * P : (g + 1) * P, :],
+                    in_=acc[:].rearrange("p t s -> p s t"),
+                    func=SILU,
+                )
 
         gather(0, P)
         gather(P, P)
+        for e in range(1, E - 1):
+            gather(e * C, C)
+        gather(S - C, P)
+        gather(S - P, P)
         for e in range(E):
-            if e + 1 < E:
-                if e + 1 >= TURNED:
-                    permute(e + 1)
-                gather((e + 1) * C, C)
+            permute(e)
             first(e)
-            if 1 <= e <= TURNED:
-                turn(e - 1)
 
-        h_scales = late.tile([P, S], U8, name="h_scales", align_bytes=64, offset=0)
+        h_scales = keep.tile([P, S], U8, name="h_scales", align_bytes=64)
+        y_banks = []
         for u, (a, n) in enumerate(UNITS):
             h_words = keep.tile([P, n * C], U32, name=f"h_words{a}", align_bytes=64)
             nc.vector.quantize_mx(
                 out=h_words[:].bitcast(FP8X4),
                 scales=h_scales[:, a * C : (a + n) * C],
-                in_=h_in[u][:].rearrange("p s j -> p (s j)"),
+                in_=h_in[u],
             )
-            if u < Y_BANKS:
-                bank = y_psum.tile([P, 4, P], F32, name="yp")
-            else:
-                bank = a_psum.tile([P, 4, P], F32, name="acc")
+            bank = psum.tile([P, 4, P], F32, name="acc")
             y_ps = bank[:].rearrange("p a b -> p (a b)")
             for i in range(n):
                 nc.tensor.matmul_mx(
@@ -268,10 +249,12 @@ def tile_moe_tk_mlp_silu_kernel(
                     start=True,
                     stop=True,
                 )
+            y_banks.append(y_ps)
+        for u, (a, n) in enumerate(UNITS):
             if u in Y_ON_VECTOR:
-                nc.vector.tensor_copy(out=y_all[:, a * C : (a + n) * C], in_=y_ps[:, 0 : n * C])
+                nc.vector.tensor_copy(out=y_all[:, a * C : (a + n) * C], in_=y_banks[u][:, 0 : n * C])
             else:
-                nc.scalar.copy(out=y_all[:, a * C : (a + n) * C], in_=y_ps[:, 0 : n * C])
+                nc.scalar.copy(out=y_all[:, a * C : (a + n) * C], in_=y_banks[u][:, 0 : n * C])
 
         def weigh(r, a, n):
             term = keep.tile([P, n], F32, name=f"term{r}_{a}")
@@ -281,8 +264,7 @@ def tile_moe_tk_mlp_silu_kernel(
             return term
 
         blocks = T // P
-        sums = [a_psum.tile([P, 4, P], F32, name="acc") for b in range(3)]
-        sums += [y_psum.tile([P, 4, P], F32, name="yp") for b in range(3)]
+        sums = [psum.tile([P, 4, P], F32, name="acc") for b in range(blocks)]
 
         def add_turned(r, a, n, last):
             term = weigh(r, a, n)
@@ -297,7 +279,7 @@ def tile_moe_tk_mlp_silu_kernel(
                 )
 
         def turn_back(a, n):
-            back = y_psum.tile([P, 512], F32, name="yp")
+            back = psum.tile([P, 512], F32, name="acc")
             for b in range(a // P, (a + n) // P):
                 sum_t = keep.tile([P, P], F32, name=f"sum_t{b}")
                 nc.scalar.copy(out=sum_t[:], in_=sums[b][:, 0, :])
@@ -310,11 +292,12 @@ def tile_moe_tk_mlp_silu_kernel(
         for a, n in BANK_TOKENS:
             add_turned(2, a, n, 2)
             three[a] = turn_back(a, n)
-        term = weigh(3, 0, T)
+        terms = {a: weigh(3, a, n) for a, n in BANK_TOKENS}
         for a, n in STORES:
             first_token = a // 512 * 512
+            at = a - first_token
             last = keep.tile([P, n], F32, name=f"last{a}")
             nc.vector.tensor_tensor(
-                last[:], term[:, a : a + n], three[first_token][:, a - first_token : a - first_token + n], ADD
+                last[:], terms[first_token][:, at : at + n], three[first_token][:, at : at + n], ADD
             )
             nc.sync.dma_start(out[:, a : a + n], last[:])

@@ -29,26 +29,27 @@ PACKS = [(0, 8), (8, 4)]
 LIVE_ROWS = 100
 LOADS = [
     ("x", 0, 0),
-    ("pack", 0, 0),
     ("x", 1, 0),
     ("x", 2, 0),
     ("x", 3, 0),
+    ("pack", 0, 0),
     ("offs", 0, 0),
-    ("w1", 0, 1),
-    ("w1", 1, 3),
-    ("shift", 1, 3),
-    ("w1", 3, 6),
-    ("shift", 3, 6),
+    ("w1", 0, 2),
+    ("w1", 2, 4),
+    ("w1", 4, 6),
     ("pack", 1, 0),
+    ("shift", 1, 3),
     ("w1", 6, 9),
-    ("shift", 6, 8),
+    ("shift", 3, 5),
     ("w1", 9, 12),
+    ("shift", 5, 8),
     ("s2", 0, 12),
     ("w2", 0, 12),
     ("shift", 9, 12),
 ]
+EARLY = 10
 BANK_TOKENS = [(0, 512), (512, 256)]
-STORES = [(0, 256), (256, 256), (512, 256)]
+STORES = [(0, 256), (256, 256), (512, 128), (640, 128)]
 
 
 def tile_moe_tk_mlp_silu_kernel(
@@ -66,7 +67,7 @@ def tile_moe_tk_mlp_silu_kernel(
         nc.vector.memset(warm[:], 0.0)
         nc.scalar.activation(out=warm_out[:], in_=warm[:], func=SILU)
 
-        w1_s, packs = {}, {}
+        w1_s, packs, raw_packs = {}, {}, {}
         w2_s = keep.tile([P, E, N], U8, name="w2_s", align_bytes=64)
         x_scales = keep.tile([P, T], U8, name="x_scales", align_bytes=64)
         nc.gpsimd.memset(x_scales[:], 0)
@@ -77,6 +78,14 @@ def tile_moe_tk_mlp_silu_kernel(
         x_view = xT.rearrange("(p j) t -> p j t", j=4)
         x_raw = {}
         raw_w, w2 = {}, {}
+
+        def permute_pack(a):
+            packs[a] = late.tile([P, H], U8, name=f"pack{a}", align_bytes=64, offset=2 * H + 64 + a * H)
+            nc.gpsimd.tensor_copy(
+                out=packs[a][:].rearrange("p (t m) -> p t m", t=4),
+                in_=raw_packs[a][:].rearrange("p (m t) -> p t m", t=4),
+            )
+            w1_s[PACKS[a][0]] = packs[a]
 
         def load(kind, a, b):
             if kind == "offs":
@@ -94,14 +103,10 @@ def tile_moe_tk_mlp_silu_kernel(
                 for q in range(4):
                     rows = w1_scales[e0 : e0 + count, 0, 4 * q : 4 * q + 4, :]
                     nc.sync.dma_start(raw[32 * q : 32 * q + 4 * count].bitcast(I32), rows.bitcast(I32))
-                packs[a] = keep.tile([P, H], U8, name=f"pack{a}", align_bytes=64)
-                engine = nc.vector if a == 0 else nc.gpsimd
-                engine.tensor_copy(
-                    out=packs[a][:].rearrange("p (t m) -> p t m", t=4),
-                    in_=raw[:].rearrange("p (m t) -> p t m", t=4),
-                )
-                w1_s[e0] = packs[a]
+                raw_packs[a] = raw
             elif kind == "shift":
+                if a // 8 not in packs:
+                    permute_pack(a // 8)
                 for e in range(a, b):
                     plane = keep.tile([P, H], U8, name=f"w1_plane{e}", align_bytes=64)
                     nc.vector.memset(plane[:].bitcast(I32), 0)
@@ -126,37 +131,14 @@ def tile_moe_tk_mlp_silu_kernel(
                 for e in range(a, b):
                     w2[e] = words[:, e - a, :]
 
-        for kind, a, b in LOADS:
+        for kind, a, b in LOADS[:EARLY]:
             load(kind, a, b)
-        pos_t = []
-        for r, pos in enumerate((pos1, pos2, pos3, pos4)):
-            lst = lists.tile([P, T // 16], U16, name=f"pos_t{r}")
-            nc.sync.dma_start(lst[:], pos)
-            pos_t.append(lst)
-        gates = []
-        for r in range(TOP):
-            g_t = keep.tile([P, T], F32, name=f"gate_t{r}")
-            nc.sync.dma_start(g_t[:], gate[r])
-            gates.append(g_t)
-
-        w1 = {}
-
-        def permute(e):
-            words, at = raw_w[e]
-            if e == 0:
-                w1[e] = late.tile([P, 2 * H], U8, name="w1_words_first", align_bytes=64, offset=0)
-            else:
-                w1[e] = keep.tile([P, 2 * H], U8, name=f"w1_words_p{e}", align_bytes=64)
-            nc.gpsimd.tensor_copy(
-                out=w1[e][:].bitcast(U16).rearrange("p (t m) -> p t m", t=4),
-                in_=words[:, at, :].bitcast(U16).rearrange("p (m t) -> p t m", t=4),
-            )
 
         x_words = keep.tile([P, T], U32, name="x_words", align_bytes=64)
         x_bf = []
         for i, (a, n) in enumerate(X_CHUNKS):
             if i == len(X_CHUNKS) - 1:
-                xb = late.tile([P, n, 4], BF16, name=f"x_bf{i}", align_bytes=64, offset=0)
+                xb = late.tile([P, n, 4], BF16, name=f"x_bf{i}", align_bytes=64, offset=2 * H)
             else:
                 xb = keep.tile([P, n, 4], BF16, name=f"x_bf{i}", align_bytes=64)
             x_bf.append(xb)
@@ -178,6 +160,32 @@ def tile_moe_tk_mlp_silu_kernel(
         for i in range(len(X_CHUNKS)):
             cast(i)
             quantise_x(i)
+
+        for kind, a, b in LOADS[EARLY:]:
+            load(kind, a, b)
+        pos_t = []
+        for r, pos in enumerate((pos1, pos2, pos3, pos4)):
+            lst = lists.tile([P, T // 16], U16, name=f"pos_t{r}")
+            nc.sync.dma_start(lst[:], pos)
+            pos_t.append(lst)
+        gates = []
+        for r in range(TOP):
+            g_t = keep.tile([P, T], F32, name=f"gate_t{r}")
+            nc.sync.dma_start(g_t[:], gate[r])
+            gates.append(g_t)
+
+        w1 = {}
+
+        def permute(e):
+            words, at = raw_w[e]
+            if e == 1:
+                w1[e] = late.tile([P, 2 * H], U8, name="w1_words_first", align_bytes=64, offset=64)
+            else:
+                w1[e] = keep.tile([P, 2 * H], U8, name=f"w1_words_p{e}", align_bytes=64)
+            nc.gpsimd.tensor_copy(
+                out=w1[e][:].bitcast(U16).rearrange("p (t m) -> p t m", t=4),
+                in_=words[:, at, :].bitcast(U16).rearrange("p (m t) -> p t m", t=4),
+            )
 
         g_words, g_scales = {}, {}
 
@@ -218,13 +226,45 @@ def tile_moe_tk_mlp_silu_kernel(
                     func=SILU,
                 )
 
+        def first_turned(e):
+            words, at = raw_w[e]
+            turned = []
+            for g in range(2):
+                acc = psum.tile([P, H], F32, name="acc")
+                nc.tensor.matmul_mx(
+                    out=acc[:],
+                    lhsT=g_words[2 * e + g].bitcast(FP8X4),
+                    lhsT_scale=g_scales[2 * e + g],
+                    rhs=words[:, at, :].bitcast(FP4X4),
+                    rhs_scale=raw_packs[0][:],
+                    start=True,
+                    stop=True,
+                )
+                h = keep.tile([P, H], BF16, name=f"h_slots{g}", align_bytes=64)
+                nc.scalar.activation(
+                    out=h[:].rearrange("s (u p e) -> s u p e", u=2, e=2),
+                    in_=acc[:].rearrange("s (p u e) -> s u p e", u=2, e=2),
+                    func=SILU,
+                )
+                turned.append(h)
+            bank = psum.tile([P, 2, 2, P], F32, name="acc")
+            for g in range(2):
+                pairs = turned[g][:].bitcast(F32)
+                for u in range(2):
+                    nc.tensor.transpose(bank[:, g, u, :], pairs[:, u * P : (u + 1) * P], ident[:])
+            nc.scalar.copy(
+                out=h_in[0][:, 0 : 4 * C].bitcast(F32).rearrange("p (g r u) -> p g r u", g=2, u=2),
+                in_=bank[:].rearrange("p g u r -> p g r u"),
+            )
+
         gather(0, P)
         gather(P, P)
         for e in range(1, E - 1):
             gather(e * C, C)
         gather(S - C, P)
         gather(S - P, P)
-        for e in range(E):
+        first_turned(0)
+        for e in range(1, E):
             permute(e)
             first(e)
 

@@ -23,7 +23,8 @@ ADD = mybir.AluOpType.add
 
 X_CHUNKS = [(0, 256), (256, 256), (512, 128), (640, 128)]
 X_ON_VECTOR = (128, 128, 80, 80)
-UNITS = [(0, 2), (2, 2), (4, 2), (6, 2), (8, 2), (10, 1), (11, 1)]
+UNITS = [(0, 8), (1, 2), (3, 4), (5, 6), (10, 11), (7,), (9,)]
+ORDER = [e for unit in UNITS for e in unit]
 Y_ON_VECTOR = (4,)
 PACKS = [(0, 8), (8, 4)]
 LIVE_ROWS = 100
@@ -34,21 +35,25 @@ LOADS = [
     ("x", 3, 0),
     ("pack", 0, 0),
     ("offs", 0, 0),
-    ("w1", 0, 2),
-    ("w1", 2, 4),
-    ("w1", 4, 6),
+    ("w1", 0, 1),
     ("pack", 1, 0),
+    ("w1", 8, 9),
+    ("w1", 1, 3),
+    ("w1", 3, 6),
     ("shift", 1, 3),
-    ("w1", 6, 9),
+    ("w1", 6, 8),
     ("shift", 3, 5),
     ("w1", 9, 12),
-    ("shift", 5, 8),
+    ("shift", 5, 7),
+    ("shift", 10, 12),
     ("s2", 0, 12),
     ("w2", 0, 12),
-    ("shift", 9, 12),
+    ("shift", 7, 8),
+    ("shift", 9, 10),
 ]
-EARLY = 10
-BANK_TOKENS = [(0, 512), (512, 256)]
+EARLY = 11
+BANK_TOKENS = [(0, 256), (256, 256), (512, 256)]
+LAST_TERMS = [(0, 512), (512, 256)]
 STORES = [(0, 256), (256, 256), (512, 128), (640, 128)]
 
 
@@ -105,8 +110,6 @@ def tile_moe_tk_mlp_silu_kernel(
                     nc.sync.dma_start(raw[32 * q : 32 * q + 4 * count].bitcast(I32), rows.bitcast(I32))
                 raw_packs[a] = raw
             elif kind == "shift":
-                if a // 8 not in packs:
-                    permute_pack(a // 8)
                 for e in range(a, b):
                     plane = keep.tile([P, H], U8, name=f"w1_plane{e}", align_bytes=64)
                     nc.vector.memset(plane[:].bitcast(I32), 0)
@@ -161,6 +164,8 @@ def tile_moe_tk_mlp_silu_kernel(
             cast(i)
             quantise_x(i)
 
+        permute_pack(0)
+        permute_pack(1)
         for kind, a, b in LOADS[EARLY:]:
             load(kind, a, b)
         pos_t = []
@@ -178,7 +183,7 @@ def tile_moe_tk_mlp_silu_kernel(
 
         def permute(e):
             words, at = raw_w[e]
-            if e == 1:
+            if e == ORDER[1]:
                 w1[e] = late.tile([P, 2 * H], U8, name="w1_words_first", align_bytes=64, offset=64)
             else:
                 w1[e] = keep.tile([P, 2 * H], U8, name=f"w1_words_p{e}", align_bytes=64)
@@ -199,12 +204,12 @@ def tile_moe_tk_mlp_silu_kernel(
                 g_scales[(a + s) // P] = scales[:, s : s + P]
 
         y_all = keep.tile([P, S], F32, name="y_all", align_bytes=64)
-        h_in = [keep.tile([P, n * C * 4], BF16, name=f"h_in{a}", align_bytes=64)[:] for a, n in UNITS[:-1]]
-        h_in.append(y_all[:, 8 * C : 10 * C].bitcast(BF16))
+        h_in = [keep.tile([P, len(unit) * C * 4], BF16, name=f"h_in{unit[0]}", align_bytes=64)[:] for unit in UNITS[:-1]]
+        h_in.append(y_all[:, 10 * C : 12 * C].bitcast(BF16))
 
         def hidden(e):
-            u = [i for i, (a, n) in enumerate(UNITS) if a <= e < a + n][0]
-            at = (e - UNITS[u][0]) * C
+            u = [i for i, unit in enumerate(UNITS) if e in unit][0]
+            at = UNITS[u].index(e) * C
             return h_in[u][:, 4 * at : 4 * (at + C)].rearrange("p (s j) -> p s j", j=4)
 
         def first(e):
@@ -259,42 +264,38 @@ def tile_moe_tk_mlp_silu_kernel(
 
         gather(0, P)
         gather(P, P)
-        for e in range(1, E - 1):
+        for e in ORDER[1:-1]:
             gather(e * C, C)
-        gather(S - C, P)
-        gather(S - P, P)
+        gather(ORDER[-1] * C, P)
+        gather(ORDER[-1] * C + P, P)
         first_turned(0)
-        for e in range(1, E):
+        for e in ORDER[1:]:
             permute(e)
             first(e)
 
-        h_scales = keep.tile([P, S], U8, name="h_scales", align_bytes=64)
         y_banks = []
-        for u, (a, n) in enumerate(UNITS):
-            h_words = keep.tile([P, n * C], U32, name=f"h_words{a}", align_bytes=64)
-            nc.vector.quantize_mx(
-                out=h_words[:].bitcast(FP8X4),
-                scales=h_scales[:, a * C : (a + n) * C],
-                in_=h_in[u],
-            )
-            bank = psum.tile([P, 4, P], F32, name="acc")
-            y_ps = bank[:].rearrange("p a b -> p (a b)")
-            for i in range(n):
+        for u, unit in enumerate(UNITS):
+            n = len(unit)
+            h_words = keep.tile([P, n * C], U32, name=f"h_words{u}", align_bytes=64)
+            h_scales = keep.tile([P, n * C], U8, name=f"h_scales{u}", align_bytes=64)
+            nc.vector.quantize_mx(out=h_words[:].bitcast(FP8X4), scales=h_scales[:], in_=h_in[u])
+            bank = psum.tile([P, 2, C], F32, name="acc")
+            for i, e in enumerate(unit):
                 nc.tensor.matmul_mx(
-                    out=y_ps[:, i * C : (i + 1) * C],
-                    lhsT=w2[a + i].bitcast(FP4X4),
-                    lhsT_scale=w2_s[:, a + i, :],
+                    out=bank[:, i, :],
+                    lhsT=w2[e].bitcast(FP4X4),
+                    lhsT_scale=w2_s[:, e, :],
                     rhs=h_words[:, i * C : (i + 1) * C].bitcast(FP8X4),
-                    rhs_scale=h_scales[:, (a + i) * C : (a + i + 1) * C],
+                    rhs_scale=h_scales[:, i * C : (i + 1) * C],
                     start=True,
                     stop=True,
                 )
-            y_banks.append(y_ps)
-        for u, (a, n) in enumerate(UNITS):
-            if u in Y_ON_VECTOR:
-                nc.vector.tensor_copy(out=y_all[:, a * C : (a + n) * C], in_=y_banks[u][:, 0 : n * C])
-            else:
-                nc.scalar.copy(out=y_all[:, a * C : (a + n) * C], in_=y_banks[u][:, 0 : n * C])
+            y_banks.append(bank)
+        y_by_expert = y_all[:].rearrange("p (e c) -> p e c", c=C)
+        for u, unit in enumerate(UNITS):
+            step = max(unit[-1] - unit[0], 1)
+            copy = nc.vector.tensor_copy if u in Y_ON_VECTOR else nc.scalar.copy
+            copy(out=y_by_expert[:, unit[0] : unit[-1] + 1 : step, :], in_=y_banks[u][:, 0 : len(unit), :])
 
         def weigh(r, a, n):
             term = keep.tile([P, n], F32, name=f"term{r}_{a}")
@@ -303,27 +304,26 @@ def tile_moe_tk_mlp_silu_kernel(
             )
             return term
 
-        blocks = T // P
-        sums = [psum.tile([P, 4, P], F32, name="acc") for b in range(blocks)]
+        sums = [psum.tile([P, 2, P], F32, name="acc") for a, n in BANK_TOKENS]
 
         def add_turned(r, a, n, last):
             term = weigh(r, a, n)
             for b in range(a // P, (a + n) // P):
                 nc.tensor.matmul(
-                    sums[b][:, 0, :],
+                    sums[b // 2][:, b % 2, :],
                     lhsT=term[:, b * P - a : (b + 1) * P - a],
                     rhs=ident[:],
                     is_transpose=True,
-                    start=r == 0,
-                    stop=r == last,
+                    start=r == 0 and b % 2 == 0,
+                    stop=r == last and b % 2 == 1,
                 )
 
         def turn_back(a, n):
             back = psum.tile([P, 512], F32, name="acc")
-            for b in range(a // P, (a + n) // P):
-                sum_t = keep.tile([P, P], F32, name=f"sum_t{b}")
-                nc.scalar.copy(out=sum_t[:], in_=sums[b][:, 0, :])
-                nc.tensor.transpose(back[:, b * P - a : (b + 1) * P - a], sum_t[:], ident[:])
+            sum_t = keep.tile([P, 2, P], F32, name=f"sum_t{a}")
+            nc.scalar.copy(out=sum_t[:], in_=sums[a // 256][:])
+            for b in range(2):
+                nc.tensor.transpose(back[:, b * P : (b + 1) * P], sum_t[:, b, :], ident[:])
             return back
 
         add_turned(0, 0, T, 2)
@@ -332,12 +332,14 @@ def tile_moe_tk_mlp_silu_kernel(
         for a, n in BANK_TOKENS:
             add_turned(2, a, n, 2)
             three[a] = turn_back(a, n)
-        terms = {a: weigh(3, a, n) for a, n in BANK_TOKENS}
+        terms = {a: weigh(3, a, n) for a, n in LAST_TERMS}
         for a, n in STORES:
             first_token = a // 512 * 512
             at = a - first_token
+            bank_token = a // 256 * 256
+            in_bank = a - bank_token
             last = keep.tile([P, n], F32, name=f"last{a}")
             nc.vector.tensor_tensor(
-                last[:], terms[first_token][:, at : at + n], three[first_token][:, at : at + n], ADD
+                last[:], terms[first_token][:, at : at + n], three[bank_token][:, in_bank : in_bank + n], ADD
             )
             nc.sync.dma_start(out[:, a : a + n], last[:])

@@ -147,10 +147,11 @@ def tile_moe_tk_mlp_silu_kernel(
             x_bf.append(xb)
 
         def cast(i):
-            src = x_raw[i][:].rearrange("p j t -> p t j")
-            cut = X_ON_VECTOR[i]
-            nc.vector.tensor_copy(out=x_bf[i][:, 0:cut, :], in_=src[:, 0:cut, :])
-            nc.scalar.copy(out=x_bf[i][:, cut:, :], in_=src[:, cut:, :])
+            src = x_raw[i][:].rearrange("p j (c t) -> p c j t", t=4)
+            dst = x_bf[i][:].rearrange("p (c t) j -> p c j t", t=4)
+            cut = X_ON_VECTOR[i] // 4
+            nc.vector.tensor_copy(out=dst[:, 0:cut], in_=src[:, 0:cut])
+            nc.scalar.copy(out=dst[:, cut:], in_=src[:, cut:])
 
         def quantise_x(i):
             a, n = X_CHUNKS[i]
@@ -226,8 +227,8 @@ def tile_moe_tk_mlp_silu_kernel(
                         stop=True,
                     )
                 nc.scalar.activation(
-                    out=hidden(e)[:, g * P : (g + 1) * P, :],
-                    in_=acc[:].rearrange("p t s -> p s t"),
+                    out=hidden(e)[:, g * P : (g + 1) * P, :].rearrange("p (c i) t -> p c t i", i=4),
+                    in_=acc[:].rearrange("p t (c i) -> p c t i", i=4),
                     func=SILU,
                 )
 

@@ -18,6 +18,7 @@ U8 = mybir.dt.uint8
 FP8X4 = mybir.dt.float8_e4m3fn_x4
 FP4X4 = mybir.dt.float4_e2m1fn_x4
 SILU = mybir.ActivationFunctionType.Silu
+COPY = mybir.ActivationFunctionType.Copy
 MULT = mybir.AluOpType.mult
 ADD = mybir.AluOpType.add
 
@@ -52,9 +53,8 @@ LOADS = [
     ("shift", 9, 10),
 ]
 EARLY = 11
-BANK_TOKENS = [(0, 256), (256, 256), (512, 256)]
-LAST_TERMS = [(0, 512), (512, 256)]
-STORES = [(0, 256), (256, 256), (512, 128), (640, 128)]
+W = 256
+BLOCKS = [0, 256, 512]
 
 
 def tile_moe_tk_mlp_silu_kernel(
@@ -174,11 +174,8 @@ def tile_moe_tk_mlp_silu_kernel(
             lst = lists.tile([P, T // 16], U16, name=f"pos_t{r}")
             nc.sync.dma_start(lst[:], pos)
             pos_t.append(lst)
-        gates = []
-        for r in range(TOP):
-            g_t = keep.tile([P, T], F32, name=f"gate_t{r}")
-            nc.sync.dma_start(g_t[:], gate[r])
-            gates.append(g_t)
+        gate_t = keep.tile([P, TOP, T], F32, name="gate_t")
+        nc.sync.dma_start(gate_t[:], gate.rearrange("r p t -> p r t"))
 
         w1 = {}
 
@@ -298,49 +295,82 @@ def tile_moe_tk_mlp_silu_kernel(
             copy = nc.vector.tensor_copy if u in Y_ON_VECTOR else nc.scalar.copy
             copy(out=y_by_expert[:, unit[0] : unit[-1] + 1 : step, :], in_=y_banks[u][:, 0 : len(unit), :])
 
-        def weigh(r, a, n):
-            term = keep.tile([P, n], F32, name=f"term{r}_{a}")
-            nc.vector.tensor_tensor(
-                term[:], y_all[:].indirect(pos_t[r][:, a // 16 : (a + n) // 16]), gates[r][:, a : a + n], MULT
-            )
+        def offsets(r, a, n):
+            return pos_t[r][:, a // 16 : (a + n) // 16]
+
+        def weigh(term, r, a, n):
+            nc.vector.tensor_tensor(term[:], y_all[:].indirect(offsets(r, a, n)), gate_t[:, r, a : a + n], MULT)
             return term
 
-        sums = [psum.tile([P, 2, P], F32, name="acc") for a, n in BANK_TOKENS]
+        def fetch(dst, r, a, n):
+            nc.scalar.activation(out=dst, in_=y_all[:].indirect(offsets(r, a, n)), func=COPY)
 
-        def add_turned(r, a, n, last):
-            term = weigh(r, a, n)
-            for b in range(a // P, (a + n) // P):
+        sums = [psum.tile([P, 2, P], F32, name="acc") for i in range(2)]
+
+        def add_turned(term, i, first, last):
+            for b in range(2):
                 nc.tensor.matmul(
-                    sums[b // 2][:, b % 2, :],
-                    lhsT=term[:, b * P - a : (b + 1) * P - a],
+                    sums[i][:, b, :],
+                    lhsT=term[:, b * P : (b + 1) * P],
                     rhs=ident[:],
                     is_transpose=True,
-                    start=r == 0 and b % 2 == 0,
-                    stop=r == last and b % 2 == 1,
+                    start=first and b == 0,
+                    stop=last and b == 1,
                 )
 
-        def turn_back(a, n):
+        def turn_back(i):
             back = psum.tile([P, 512], F32, name="acc")
-            sum_t = keep.tile([P, 2, P], F32, name=f"sum_t{a}")
-            nc.scalar.copy(out=sum_t[:], in_=sums[a // 256][:])
+            sum_t = keep.tile([P, 2, P], F32, name=f"sum_t{i}")
+            nc.scalar.copy(out=sum_t[:], in_=sums[i][:])
             for b in range(2):
                 nc.tensor.transpose(back[:, b * P : (b + 1) * P], sum_t[:, b, :], ident[:])
             return back
 
-        add_turned(0, 0, T, 2)
-        add_turned(1, 0, T, 2)
-        three = {}
-        for a, n in BANK_TOKENS:
-            add_turned(2, a, n, 2)
-            three[a] = turn_back(a, n)
-        terms = {a: weigh(3, a, n) for a, n in LAST_TERMS}
-        for a, n in STORES:
-            first_token = a // 512 * 512
-            at = a - first_token
-            bank_token = a // 256 * 256
-            in_bank = a - bank_token
-            last = keep.tile([P, n], F32, name=f"last{a}")
-            nc.vector.tensor_tensor(
-                last[:], terms[first_token][:, at : at + n], three[bank_token][:, in_bank : in_bank + n], ADD
-            )
-            nc.sync.dma_start(out[:, a : a + n], last[:])
+        plain, terms = {}, {}
+
+        def fetch_into(dst, i, r):
+            plain[i, r] = dst
+            fetch(dst[:], r, BLOCKS[i], W)
+
+        def term(i, r, on=None):
+            a = BLOCKS[i]
+            terms[i, r] = on if on is not None else keep.tile([P, W], F32, name=f"term{r}_{a}")
+            if (i, r) in plain:
+                nc.vector.tensor_tensor(terms[i, r][:], plain[i, r][:], gate_t[:, r, a : a + W], MULT)
+            else:
+                weigh(terms[i, r], r, a, W)
+            return terms[i, r]
+
+        def store(a, n, values):
+            nc.sync.dma_start(out[:, a : a + n], values)
+
+        for i, r in [(0, 0), (0, 1), (1, 0), (1, 1), (2, 0)]:
+            fetch_into(keep.tile([P, W], F32, name=f"fetched{i}_{r}"), i, r)
+        for r in (2, 3, 0, 1):
+            add_turned(term(0, r), 0, r == 2, r == 1)
+        add_turned(term(1, 2, plain[0, 0]), 1, True, False)
+        add_turned(term(1, 0), 1, False, False)
+        add_turned(term(1, 3, plain[0, 1]), 1, False, False)
+        add_turned(term(1, 1), 1, False, True)
+        back0 = turn_back(0)
+        fetch_into(terms[0, 1], 2, 1)
+        fetch_into(terms[1, 2], 2, 2)
+        back1 = turn_back(1)
+        nc.scalar.copy(out=terms[1, 1][:], in_=back0[:, 0:W])
+        store(BLOCKS[0], W, terms[1, 1][:])
+        whole = keep.tile([P, W], F32, name="whole")
+        for at in (0, P):
+            nc.scalar.copy(out=whole[:, at : at + P], in_=back1[:, at : at + P])
+            store(BLOCKS[1] + at, P, whole[:, at : at + P])
+
+        c0, c3, c1 = term(2, 0), term(2, 3, plain[1, 0]), term(2, 1)
+        two = keep.tile([P, W], F32, name="two")
+        nc.vector.tensor_tensor(two[:], c0[:], c3[:], ADD)
+        c2 = term(2, 2)
+        three = keep.tile([P, W], F32, name="three")
+        four = keep.tile([P, W], F32, name="four")
+        for at in (0, P):
+            nc.vector.tensor_tensor(three[:, at : at + P], two[:, at : at + P], c1[:, at : at + P], ADD)
+        for at in (0, P):
+            nc.vector.tensor_tensor(four[:, at : at + P], three[:, at : at + P], c2[:, at : at + P], ADD)
+            store(BLOCKS[2] + at, P, four[:, at : at + P])

@@ -224,8 +224,8 @@ def tile_moe_tk_mlp_silu_kernel(
                         stop=True,
                     )
                 nc.scalar.activation(
-                    out=hidden(e)[:, g * P : (g + 1) * P, :].rearrange("p (c i) t -> p c t i", i=4),
-                    in_=acc[:].rearrange("p t (c i) -> p c t i", i=4),
+                    out=hidden(e)[:, g * P : (g + 1) * P, :].rearrange("p (c i) t -> p c t i", i=2),
+                    in_=acc[:].rearrange("p t (c i) -> p c t i", i=2),
                     func=SILU,
                 )
 
@@ -361,7 +361,7 @@ def tile_moe_tk_mlp_silu_kernel(
         whole = keep.tile([P, W], F32, name="whole")
         for at in (0, P):
             nc.scalar.copy(out=whole[:, at : at + P], in_=back1[:, at : at + P])
-            store(BLOCKS[1] + at, P, whole[:, at : at + P])
+            nc.scalar.dma_start(out[:, BLOCKS[1] + at : BLOCKS[1] + at + P], whole[:, at : at + P])
 
         c0, c3, c1 = term(2, 0), term(2, 3, plain[1, 0]), term(2, 1)
         two = keep.tile([P, W], F32, name="two")

@@ -305,25 +305,26 @@ def tile_moe_tk_mlp_silu_kernel(
         def fetch(dst, r, a, n):
             nc.scalar.activation(out=dst, in_=y_all[:].indirect(offsets(r, a, n)), func=COPY)
 
-        sums = [psum.tile([P, 2, P], F32, name="acc") for i in range(2)]
+        sum0 = psum.tile([P, 2, P], F32, name="acc")
+        sum1 = [psum.tile([P, P], F32, name="acc") for b in range(2)]
 
         def add_turned(term, i, first, last):
             for b in range(2):
                 nc.tensor.matmul(
-                    sums[i][:, b, :],
+                    sum0[:, b, :] if i == 0 else sum1[b][:],
                     lhsT=term[:, b * P : (b + 1) * P],
                     rhs=ident[:],
                     is_transpose=True,
-                    start=first and b == 0,
-                    stop=last and b == 1,
+                    start=first and (b == 0 or i == 1),
+                    stop=last and (b == 1 or i == 1),
                 )
 
-        def turn_back(i):
-            back = psum.tile([P, 512], F32, name="acc")
-            sum_t = keep.tile([P, 2, P], F32, name=f"sum_t{i}")
-            nc.scalar.copy(out=sum_t[:], in_=sums[i][:])
-            for b in range(2):
-                nc.tensor.transpose(back[:, b * P : (b + 1) * P], sum_t[:, b, :], ident[:])
+        def turn_back(name, summed, n):
+            back = psum.tile([P, n, P], F32, name="acc")
+            sum_t = keep.tile([P, n, P], F32, name=name)
+            nc.scalar.copy(out=sum_t[:], in_=summed)
+            for b in range(n):
+                nc.tensor.transpose(back[:, b, :], sum_t[:, b, :], ident[:])
             return back
 
         plain, terms = {}, {}
@@ -352,15 +353,15 @@ def tile_moe_tk_mlp_silu_kernel(
         add_turned(term(1, 0), 1, False, False)
         add_turned(term(1, 3, plain[0, 1]), 1, False, False)
         add_turned(term(1, 1), 1, False, True)
-        back0 = turn_back(0)
+        back0 = turn_back("sum_t0", sum0[:], 2)
         fetch_into(terms[0, 1], 2, 1)
         fetch_into(terms[1, 2], 2, 2)
-        back1 = turn_back(1)
-        nc.scalar.copy(out=terms[1, 1][:], in_=back0[:, 0:W])
+        back1 = [turn_back(f"sum_t1{b}", sum1[b][:].unsqueeze(1), 1) for b in range(2)]
+        nc.scalar.copy(out=terms[1, 1][:], in_=back0[:].rearrange("p b m -> p (b m)"))
         store(BLOCKS[0], W, terms[1, 1][:])
         whole = keep.tile([P, W], F32, name="whole")
         for at in (0, P):
-            nc.scalar.copy(out=whole[:, at : at + P], in_=back1[:, at : at + P])
+            nc.scalar.copy(out=whole[:, at : at + P], in_=back1[at // P][:, 0, :])
             nc.scalar.dma_start(out[:, BLOCKS[1] + at : BLOCKS[1] + at + P], whole[:, at : at + P])
 
         c0, c3, c1 = term(2, 0), term(2, 3, plain[1, 0]), term(2, 1)

@@ -22,8 +22,9 @@ COPY = mybir.ActivationFunctionType.Copy
 MULT = mybir.AluOpType.mult
 ADD = mybir.AluOpType.add
 
-X_CHUNKS = [(0, 256), (256, 256), (512, 128), (640, 128)]
-X_ON_VECTOR = (128, 128, 80, 80)
+X_LOADS = [(0, 256), (256, 256), (512, 128), (640, 128)]
+X_CHUNKS = [(0, 256), (256, 128), (384, 128), (512, 128), (640, 128)]
+X_ON_VECTOR = (128, 80, 80, 0, 96)
 UNITS = [(0, 8), (1, 2), (3, 4), (5, 6), (10, 11), (7,), (9,)]
 ORDER = [e for unit in UNITS for e in unit]
 Y_ON_VECTOR = (4,)
@@ -96,10 +97,12 @@ def tile_moe_tk_mlp_silu_kernel(
             if kind == "offs":
                 nc.sync.dma_start(offs_t[:], offs)
             elif kind == "x":
-                raw = keep.tile([P, 4, X_CHUNKS[a][1]], F32, name=f"x_raw{a}")
-                c = X_CHUNKS[a][0]
-                nc.sync.dma_start(raw[:], x_view[:, :, c : c + X_CHUNKS[a][1]])
-                x_raw[a] = raw
+                c0, width = X_LOADS[a]
+                raw = keep.tile([P, 4, width], F32, name=f"x_raw{a}")
+                nc.sync.dma_start(raw[:], x_view[:, :, c0 : c0 + width])
+                for i, (c, n) in enumerate(X_CHUNKS):
+                    if c0 <= c < c0 + width:
+                        x_raw[i] = raw[:, :, c - c0 : c - c0 + n]
             elif kind == "pack":
                 e0, count = PACKS[a]
                 raw = keep.tile([P, H], U8, name=f"raw_pack{a}", align_bytes=64)
@@ -147,10 +150,11 @@ def tile_moe_tk_mlp_silu_kernel(
             x_bf.append(xb)
 
         def cast(i):
-            src = x_raw[i][:].rearrange("p j (c t) -> p c j t", t=4)
+            src = x_raw[i].rearrange("p j (c t) -> p c j t", t=4)
             dst = x_bf[i][:].rearrange("p (c t) j -> p c j t", t=4)
             cut = X_ON_VECTOR[i] // 4
-            nc.vector.tensor_copy(out=dst[:, 0:cut], in_=src[:, 0:cut])
+            if cut:
+                nc.vector.tensor_copy(out=dst[:, 0:cut], in_=src[:, 0:cut])
             nc.scalar.copy(out=dst[:, cut:], in_=src[:, cut:])
 
         def quantise_x(i):

@@ -24,7 +24,7 @@ ADD = mybir.AluOpType.add
 
 X_LOADS = [(0, 256), (256, 256), (512, 128), (640, 128)]
 X_CHUNKS = [(0, 256), (256, 128), (384, 128), (512, 128), (640, 128)]
-X_ON_VECTOR = (128, 80, 80, 0, 96)
+X_ON_VECTOR = (128, 80, 80, 0, 72)
 UNITS = [(0, 8), (1, 2), (3, 4), (5, 6), (10, 11), (7,), (9,)]
 ORDER = [e for unit in UNITS for e in unit]
 Y_ON_VECTOR = (4,)
@@ -38,8 +38,8 @@ LOADS = [
     ("pack", 0, 0),
     ("offs", 0, 0),
     ("w1", 0, 1),
-    ("pack", 1, 0),
     ("w1", 8, 9),
+    ("pack", 1, 0),
     ("w1", 1, 3),
     ("w1", 3, 6),
     ("shift", 1, 3),
@@ -185,11 +185,12 @@ def tile_moe_tk_mlp_silu_kernel(
 
         def permute(e):
             words, at = raw_w[e]
-            if e == ORDER[1]:
+            if e == ORDER[2]:
                 w1[e] = late.tile([P, 2 * H], U8, name="w1_words_first", align_bytes=64, offset=64)
             else:
                 w1[e] = keep.tile([P, 2 * H], U8, name=f"w1_words_p{e}", align_bytes=64)
-            nc.gpsimd.tensor_copy(
+            copy = nc.scalar.copy if e == ORDER[1] else nc.gpsimd.tensor_copy
+            copy(
                 out=w1[e][:].bitcast(U16).rearrange("p (t m) -> p t m", t=4),
                 in_=words[:, at, :].bitcast(U16).rearrange("p (m t) -> p t m", t=4),
             )

from contextlib import ExitStack

import concourse.mybir as mybir
from concourse.masks import make_identity

K, T, E, C, H, N = 512, 768, 12, 256, 512, 128
TOP = 4
P = 128
S = E * C
FLOPS = 2 * S * (K * H + H * N)

F32 = mybir.dt.float32
BF16 = mybir.dt.bfloat16
U32 = mybir.dt.uint32
I32 = mybir.dt.int32
U16 = mybir.dt.uint16
U8 = mybir.dt.uint8
FP8X4 = mybir.dt.float8_e4m3fn_x4
FP4X4 = mybir.dt.float4_e2m1fn_x4
SILU = mybir.ActivationFunctionType.Silu
COPY = mybir.ActivationFunctionType.Copy
MULT = mybir.AluOpType.mult
ADD = mybir.AluOpType.add

X_LOADS = [(0, 256), (256, 256), (512, 128), (640, 128)]
X_CHUNKS = [(0, 256), (256, 128), (384, 128), (512, 128), (640, 128)]
X_ON_VECTOR = (128, 80, 80, 0, 72)
UNITS = [(0, 8), (1, 2), (3, 4), (5, 6), (10, 11), (7,), (9,)]
ORDER = [e for unit in UNITS for e in unit]
Y_ON_VECTOR = (4,)
PACKS = [(0, 8), (8, 4)]
LIVE_ROWS = 100
LOADS = [
    ("x", 0, 0),
    ("x", 1, 0),
    ("x", 2, 0),
    ("x", 3, 0),
    ("pack", 0, 0),
    ("offs", 0, 0),
    ("w1", 0, 1),
    ("w1", 8, 9),
    ("pack", 1, 0),
    ("w1", 1, 3),
    ("w1", 3, 6),
    ("shift", 1, 3),
    ("w1", 6, 8),
    ("shift", 3, 5),
    ("w1", 9, 12),
    ("shift", 5, 7),
    ("shift", 10, 12),
    ("s2", 0, 12),
    ("w2", 0, 12),
    ("shift", 7, 8),
    ("shift", 9, 10),
]
EARLY = 11
W = 256
BLOCKS = [0, 256, 512]


def tile_moe_tk_mlp_silu_kernel(
    tc, xT, w1_words, w1_scales, w2_words, w2_scales, gate, offs, pos1, pos2, pos3, pos4, out
):
    nc = tc.nc
    with ExitStack() as ctx:
        lists = ctx.enter_context(tc.tile_pool(name="lists", bufs=1))
        keep = ctx.enter_context(tc.tile_pool(name="keep", bufs=1))
        late = ctx.enter_context(tc.tile_pool(name="late", bufs=1))
        psum = ctx.enter_context(tc.psum_pool(name="psum", bufs=8))

        warm = keep.tile([P, 1], F32, name="warm")
        warm_out = keep.tile([P, 1], F32, name="warm_out")
        nc.vector.memset(warm[:], 0.0)
        nc.scalar.activation(out=warm_out[:], in_=warm[:], func=SILU)

        w1_s, packs, raw_packs = {}, {}, {}
        w2_s = keep.tile([P, E, N], U8, name="w2_s", align_bytes=64)
        x_scales = keep.tile([P, T], U8, name="x_scales", align_bytes=64)
        nc.gpsimd.memset(x_scales[:], 0)
        ident = keep.tile([P, P], F32, name="ident")
        make_identity(nc, ident[:])

        offs_t = lists.tile([P, S // 16], U16, name="offs_t")
        x_view = xT.rearrange("(p j) t -> p j t", j=4)
        x_raw = {}
        raw_w, w2 = {}, {}

        def permute_pack(a):
            packs[a] = late.tile([P, H], U8, name=f"pack{a}", align_bytes=64, offset=2 * H + 64 + a * H)
            nc.gpsimd.tensor_copy(
                out=packs[a][:].rearrange("p (t m) -> p t m", t=4),
                in_=raw_packs[a][:].rearrange("p (m t) -> p t m", t=4),
            )
            w1_s[PACKS[a][0]] = packs[a]

        def load(kind, a, b):
            if kind == "offs":
                nc.sync.dma_start(offs_t[:], offs)
            elif kind == "x":
                c0, width = X_LOADS[a]
                raw = keep.tile([P, 4, width], F32, name=f"x_raw{a}")
                nc.sync.dma_start(raw[:], x_view[:, :, c0 : c0 + width])
                for i, (c, n) in enumerate(X_CHUNKS):
                    if c0 <= c < c0 + width:
                        x_raw[i] = raw[:, :, c - c0 : c - c0 + n]
            elif kind == "pack":
                e0, count = PACKS[a]
                raw = keep.tile([P, H], U8, name=f"raw_pack{a}", align_bytes=64)
                if count < 8:
                    nc.vector.memset(raw[:].bitcast(I32), 0)
                for q in range(4):
                    rows = w1_scales[e0 : e0 + count, 0, 4 * q : 4 * q + 4, :]
                    nc.sync.dma_start(raw[32 * q : 32 * q + 4 * count].bitcast(I32), rows.bitcast(I32))
                raw_packs[a] = raw
            elif kind == "shift":
                for e in range(a, b):
                    plane = keep.tile([P, H], U8, name=f"w1_plane{e}", align_bytes=64)
                    nc.vector.memset(plane[:].bitcast(I32), 0)
                    j = e % 8
                    nc.sync.dma_start(
                        plane[0:LIVE_ROWS].bitcast(I32), packs[e // 8][4 * j : 4 * j + LIVE_ROWS].bitcast(I32)
                    )
                    w1_s[e] = plane
            elif kind == "s2":
                nc.vector.memset(w2_s[:].bitcast(I32), 0)
                for q in range(4):
                    rows = w2_scales[a:b, 0, q:16:4, :].rearrange("e q n -> q e n")
                    nc.sync.dma_start(w2_s[q:P:32, a:b, :].bitcast(I32), rows.bitcast(I32))
            elif kind == "w1":
                words = keep.tile([P, b - a, 2 * H], U8, name=f"raw_w{a}", align_bytes=64)
                nc.sync.dma_start(words[:], w1_words[a:b, 0].rearrange("e p c -> p e c"))
                for e in range(a, b):
                    raw_w[e] = (words, e - a)
            else:
                words = keep.tile([P, b - a, 2 * N], U8, name=f"w2_{a}", align_bytes=64)
                nc.sync.dma_start(words[:], w2_words[a:b, 0].rearrange("e p c -> p e c"))
                for e in range(a, b):
                    w2[e] = words[:, e - a, :]

        for kind, a, b in LOADS[:EARLY]:
            load(kind, a, b)

        x_words = keep.tile([P, T], U32, name="x_words", align_bytes=64)
        x_bf = []
        for i, (a, n) in enumerate(X_CHUNKS):
            if i == len(X_CHUNKS) - 1:
                xb = late.tile([P, n, 4], BF16, name=f"x_bf{i}", align_bytes=64, offset=2 * H)
            else:
                xb = keep.tile([P, n, 4], BF16, name=f"x_bf{i}", align_bytes=64)
            x_bf.append(xb)

        def cast(i):
            src = x_raw[i].rearrange("p j (c t) -> p c j t", t=4)
            dst = x_bf[i][:].rearrange("p (c t) j -> p c j t", t=4)
            cut = X_ON_VECTOR[i] // 4
            if cut:
                nc.vector.tensor_copy(out=dst[:, 0:cut], in_=src[:, 0:cut])
            nc.scalar.copy(out=dst[:, cut:], in_=src[:, cut:])

        def quantise_x(i):
            a, n = X_CHUNKS[i]
            nc.vector.quantize_mx(
                out=x_words[:, a : a + n].bitcast(FP8X4),
                scales=x_scales[:, a : a + n],
                in_=x_bf[i][:].rearrange("p t j -> p (t j)"),
            )

        for i in range(len(X_CHUNKS)):
            cast(i)
            quantise_x(i)

        permute_pack(0)
        permute_pack(1)
        for kind, a, b in LOADS[EARLY:]:
            load(kind, a, b)
        pos_t = []
        for r, pos in enumerate((pos1, pos2, pos3, pos4)):
            lst = lists.tile([P, T // 16], U16, name=f"pos_t{r}")
            nc.sync.dma_start(lst[:], pos)
            pos_t.append(lst)
        gate_t = keep.tile([P, TOP, T], F32, name="gate_t")
        nc.sync.dma_start(gate_t[:], gate.rearrange("r p t -> p r t"))

        w1 = {}

        def permute(e):
            words, at = raw_w[e]
            if e == ORDER[2]:
                w1[e] = late.tile([P, 2 * H], U8, name="w1_words_first", align_bytes=64, offset=64)
            else:
                w1[e] = keep.tile([P, 2 * H], U8, name=f"w1_words_p{e}", align_bytes=64)
            copy = nc.scalar.copy if e == ORDER[1] else nc.gpsimd.tensor_copy
            copy(
                out=w1[e][:].bitcast(U16).rearrange("p (t m) -> p t m", t=4),
                in_=words[:, at, :].bitcast(U16).rearrange("p (m t) -> p t m", t=4),
            )

        g_words, g_scales = {}, {}

        def gather(a, n):
            words = keep.tile([P, n], U32, name=f"g_words_{a}", align_bytes=64)
            nc.vector.tensor_copy(words[:], x_words[:].indirect(offs_t[:, a // 16 : (a + n) // 16]))
            scales = keep.tile([P, n], U8, name=f"g_scales_{a}", align_bytes=64)
            nc.vector.tensor_copy(scales[:], x_scales[:].indirect(offs_t[:, a // 16 : (a + n) // 16]))
            for s in range(0, n, P):
                g_words[(a + s) // P] = words[:, s : s + P]
                g_scales[(a + s) // P] = scales[:, s : s + P]

        y_all = keep.tile([P, S], F32, name="y_all", align_bytes=64)
        h_in = [keep.tile([P, len(unit) * C * 4], BF16, name=f"h_in{unit[0]}", align_bytes=64)[:] for unit in UNITS[:-1]]
        h_in.append(y_all[:, 10 * C : 12 * C].bitcast(BF16))

        def hidden(e):
            u = [i for i, unit in enumerate(UNITS) if e in unit][0]
            at = UNITS[u].index(e) * C
            return h_in[u][:, 4 * at : 4 * (at + C)].rearrange("p (s j) -> p s j", j=4)

        def first(e):
            for g in range(2):
                acc = psum.tile([P, 4, P], F32, name="acc")
                for t in range(4):
                    nc.tensor.matmul_mx(
                        out=acc[:, t, :],
                        lhsT=w1[e][:, 2 * P * t : 2 * P * (t + 1)].bitcast(FP4X4),
                        lhsT_scale=w1_s[e][:, P * t : P * (t + 1)],
                        rhs=g_words[2 * e + g].bitcast(FP8X4),
                        rhs_scale=g_scales[2 * e + g],
                        start=True,
                        stop=True,
                    )
                nc.scalar.activation(
                    out=hidden(e)[:, g * P : (g + 1) * P, :].rearrange("p (c i) t -> p c t i", i=2),
                    in_=acc[:].rearrange("p t (c i) -> p c t i", i=2),
                    func=SILU,
                )

        def first_turned(e):
            words, at = raw_w[e]
            turned = []
            for g in range(2):
                acc = psum.tile([P, H], F32, name="acc")
                nc.tensor.matmul_mx(
                    out=acc[:],
                    lhsT=g_words[2 * e + g].bitcast(FP8X4),
                    lhsT_scale=g_scales[2 * e + g],
                    rhs=words[:, at, :].bitcast(FP4X4),
                    rhs_scale=raw_packs[0][:],
                    start=True,
                    stop=True,
                )
                h = keep.tile([P, H], BF16, name=f"h_slots{g}", align_bytes=64)
                nc.scalar.activation(
                    out=h[:].rearrange("s (u p e) -> s u p e", u=2, e=2),
                    in_=acc[:].rearrange("s (p u e) -> s u p e", u=2, e=2),
                    func=SILU,
                )
                turned.append(h)
            bank = psum.tile([P, 2, 2, P], F32, name="acc")
            for g in range(2):
                pairs = turned[g][:].bitcast(F32)
                for u in range(2):
                    nc.tensor.transpose(bank[:, g, u, :], pairs[:, u * P : (u + 1) * P], ident[:])
            nc.scalar.copy(
                out=h_in[0][:, 0 : 4 * C].bitcast(F32).rearrange("p (g r u) -> p g r u", g=2, u=2),
                in_=bank[:].rearrange("p g u r -> p g r u"),
            )

        gather(0, P)
        gather(P, P)
        for e in ORDER[1:-1]:
            gather(e * C, C)
        gather(ORDER[-1] * C, P)
        gather(ORDER[-1] * C + P, P)
        first_turned(0)
        for e in ORDER[1:]:
            permute(e)
            first(e)

        y_banks = []
        for u, unit in enumerate(UNITS):
            n = len(unit)
            h_words = keep.tile([P, n * C], U32, name=f"h_words{u}", align_bytes=64)
            h_scales = keep.tile([P, n * C], U8, name=f"h_scales{u}", align_bytes=64)
            nc.vector.quantize_mx(out=h_words[:].bitcast(FP8X4), scales=h_scales[:], in_=h_in[u])
            bank = psum.tile([P, 2, C], F32, name="acc")
            for i, e in enumerate(unit):
                nc.tensor.matmul_mx(
                    out=bank[:, i, :],
                    lhsT=w2[e].bitcast(FP4X4),
                    lhsT_scale=w2_s[:, e, :],
                    rhs=h_words[:, i * C : (i + 1) * C].bitcast(FP8X4),
                    rhs_scale=h_scales[:, i * C : (i + 1) * C],
                    start=True,
                    stop=True,
                )
            y_banks.append(bank)
        y_by_expert = y_all[:].rearrange("p (e c) -> p e c", c=C)
        for u, unit in enumerate(UNITS):
            step = max(unit[-1] - unit[0], 1)
            copy = nc.vector.tensor_copy if u in Y_ON_VECTOR else nc.scalar.copy
            copy(out=y_by_expert[:, unit[0] : unit[-1] + 1 : step, :], in_=y_banks[u][:, 0 : len(unit), :])

        def offsets(r, a, n):
            return pos_t[r][:, a // 16 : (a + n) // 16]

        def weigh(term, r, a, n):
            nc.vector.tensor_tensor(term[:], y_all[:].indirect(offsets(r, a, n)), gate_t[:, r, a : a + n], MULT)
            return term

        def fetch(dst, r, a, n):
            nc.scalar.activation(out=dst, in_=y_all[:].indirect(offsets(r, a, n)), func=COPY)

        sum0 = psum.tile([P, 2, P], F32, name="acc")
        sum1 = [psum.tile([P, P], F32, name="acc") for b in range(2)]

        def add_turned(term, i, first, last):
            for b in range(2):
                nc.tensor.matmul(
                    sum0[:, b, :] if i == 0 else sum1[b][:],
                    lhsT=term[:, b * P : (b + 1) * P],
                    rhs=ident[:],
                    is_transpose=True,
                    start=first and (b == 0 or i == 1),
                    stop=last and (b == 1 or i == 1),
                )

        def turn_back(name, summed, n):
            back = psum.tile([P, n, P], F32, name="acc")
            sum_t = keep.tile([P, n, P], F32, name=name)
            nc.scalar.copy(out=sum_t[:], in_=summed)
            for b in range(n):
                nc.tensor.transpose(back[:, b, :], sum_t[:, b, :], ident[:])
            return back

        plain, terms = {}, {}

        def fetch_into(dst, i, r):
            plain[i, r] = dst
            fetch(dst[:], r, BLOCKS[i], W)

        def term(i, r, on=None):
            a = BLOCKS[i]
            terms[i, r] = on if on is not None else keep.tile([P, W], F32, name=f"term{r}_{a}")
            if (i, r) in plain:
                nc.vector.tensor_tensor(terms[i, r][:], plain[i, r][:], gate_t[:, r, a : a + W], MULT)
            else:
                weigh(terms[i, r], r, a, W)
            return terms[i, r]

        def store(a, n, values):
            nc.sync.dma_start(out[:, a : a + n], values)

        for i, r in [(0, 0), (0, 1), (1, 0), (1, 1), (2, 0)]:
            fetch_into(keep.tile([P, W], F32, name=f"fetched{i}_{r}"), i, r)
        for r in (2, 3, 0, 1):
            add_turned(term(0, r), 0, r == 2, r == 1)
        add_turned(term(1, 2, plain[0, 0]), 1, True, False)
        add_turned(term(1, 0), 1, False, False)
        add_turned(term(1, 3, plain[0, 1]), 1, False, False)
        add_turned(term(1, 1), 1, False, True)
        back0 = turn_back("sum_t0", sum0[:], 2)
        fetch_into(terms[0, 1], 2, 1)
        fetch_into(terms[1, 2], 2, 2)
        back1 = [turn_back(f"sum_t1{b}", sum1[b][:].unsqueeze(1), 1) for b in range(2)]
        nc.scalar.copy(out=terms[1, 1][:], in_=back0[:].rearrange("p b m -> p (b m)"))
        store(BLOCKS[0], W, terms[1, 1][:])
        whole = keep.tile([P, W], F32, name="whole")
        for at in (0, P):
            nc.scalar.copy(out=whole[:, at : at + P], in_=back1[at // P][:, 0, :])
            nc.scalar.dma_start(out[:, BLOCKS[1] + at : BLOCKS[1] + at + P], whole[:, at : at + P])

        c0, c3, c1 = term(2, 0), term(2, 3, plain[1, 0]), term(2, 1)
        two = keep.tile([P, W], F32, name="two")
        nc.vector.tensor_tensor(two[:], c0[:], c3[:], ADD)
        c2 = term(2, 2)
        three = keep.tile([P, W], F32, name="three")
        four = keep.tile([P, W], F32, name="four")
        for at in (0, P):
            nc.vector.tensor_tensor(three[:, at : at + P], two[:, at : at + P], c1[:, at : at + P], ADD)
        for at in (0, P):
            nc.vector.tensor_tensor(four[:, at : at + P], three[:, at : at + P], c2[:, at : at + P], ADD)
            store(BLOCKS[2] + at, P, four[:, at : at + P])
